import numpy as np, ml_dtypes
CORES = [1,5,17,21,33,37,49,53]
N = 8
import mx_ref
BF = ml_dtypes.bfloat16
def gentries(a):
    return np.ascontiguousarray(a.reshape(8, 16, -1).transpose(0, 2, 1)).reshape(8, -1)
def gtable(e):
    e = np.asarray(e); return np.ascontiguousarray(e.reshape(8, -1, 16).transpose(0, 2, 1)).reshape(128, -1).astype(np.int32)
def gcols(t, e):
    v = np.concatenate([t.reshape(8, 16, -1, 4), np.zeros((8, 16, 1, 4), BF)], axis=2)
    return np.ascontiguousarray(np.stack([v[g][:, e[g]] for g in range(8)])).reshape(128, -1)
def gpick(z, e):
    return np.concatenate([z[16 * g:16 * g + 16][:, e[g]] for g in range(8)])
def tile(rs):
    return np.stack(rs, axis=2).reshape(128, -1).astype(BF)
def pick(q, e):
    c = np.concatenate([q[0].reshape(128, -1, 4), np.zeros((128, 1, 4), np.uint8)], axis=1); s = np.concatenate([q[1], np.ones((16, 1), np.uint8)], axis=1)
    return (np.ascontiguousarray(c[:, e].reshape(128, -1)), np.ascontiguousarray(s[:, e]))
def join(*qs):
    return (np.concatenate([q[0] for q in qs], axis=1), np.concatenate([q[1] for q in qs], axis=1))
def put(q, e, v):
    c, s = q[0].reshape(128, -1, 4).copy(), q[1].copy(); c[:, e] = v[0].reshape(128, -1, 4); s[:, e] = v[1]
    return (c.reshape(128, -1), s)
def pk(c, s):
    return (np.ascontiguousarray(c), mx_ref.live(s))
def emit(q):
    return q[0], q[1]
def packed(v, rng):
    q = [mx_ref.quantize(np.ascontiguousarray(v[r])) for r in range(N)]
    return np.stack([a for a, b in q]), np.stack([mx_ref.plane(b, rng) for a, b in q])
def values_of_codes():
    e, c = np.zeros((128, 128, 4), np.float32), np.zeros((128, 2, 4), np.uint8)
    e[np.arange(128), np.arange(128), 0] = 1
    c[:127, :, 0] = np.arange(256).reshape(2, 128).T[:127]
    return mx_ref.matmul(mx_ref.quantize(e.reshape(128, 512).astype(BF)), (c.reshape(128, 8), np.full((16, 2), 127, np.uint8))).T.reshape(-1).astype(np.float64)
CODE_VALUE, SCALE_VALUE = values_of_codes(), 2.0 ** (np.arange(256) - 127.0)
def decode(q):
    return (CODE_VALUE[q[0]].reshape(16, 8, -1, 4) * SCALE_VALUE[q[1]][:, None, :, None] + 0.0).reshape(128, -1).astype(np.float32)
def f(rng, *shape):
    return mx_ref.flush((rng.standard_normal(shape, dtype=np.float32) * np.exp2(rng.integers(-2, 3, shape[:-1] + (1,)))).astype(BF))
def wide(rng, *shape, cols=0):
    v = rng.standard_normal(shape, dtype=np.float32) * np.exp2(rng.integers(-12, 13, shape)).astype(np.float32)
    if cols: v *= np.repeat(np.exp2(rng.integers(-cols, cols + 1, shape[:-2] + (1, shape[-1] // 4))) * (rng.random(shape[:-2] + (1, shape[-1] // 4)) > 0.0625), 4, axis=-1).astype(np.float32)
    return mx_ref.flush(v.astype(BF))
C, L, M, R = 256, 6, 32, 3
def big(v):
    v = v.astype(np.float32)
    v[np.abs(v) < np.float32(2.0 ** -16)] = 0
    return v.astype(BF)
def numbers_of(rng):
    return {"x": big(f(rng, N, 128, 4 * C)), "u": np.array(f(rng, N, 128, 512)), "v": np.array(f(rng, N, 128, 512))}
def some_links(rng):
    w = rng.choice([8, 16, 32, C], (8, 1, 1))
    return (np.arange(C) + 1 + (rng.random((8, 2, C)) * w).astype(np.int64)) % C
def links_of(rng):
    return np.stack([gtable(some_links(rng).reshape(8, 2 * C)) for r in range(N)])
def layers(rng):
    return big(f(rng, N, 128, 2048)).reshape(N, 8, 16, 4, 8, 16, 4)
def weights(rng, w):
    c, p = packed(np.ascontiguousarray(w).reshape(N, 128, 2048), rng)
    return {"wc": c, "ws": p}
def setup_inputs(rng):
    return {**numbers_of(rng), "nb": links_of(rng), **weights(rng, layers(rng))}
def setup_inputs_ties(rng):
    d = numbers_of(rng)
    o = rng.permutation(N)
    k = rng.integers(-1, 3, (N, 8, C))
    k[o[1]] = rng.integers(-3, 0, (8, C))
    k[o[2]] = 1
    x = d["x"].reshape(N, 8, 16, C, 4)
    x[:, :, 0] = 0
    x[:, :, 0, :, 0] = k.astype(np.float32).astype(BF)
    u = d["u"].reshape(N, 128, 128, 4)
    u[:, :, ::16] = 0
    for h in range(0, 128, 16): u[:, h, h, 0] = 1
    u[o[0], :, ::16] = 0
    w = layers(rng)
    w[:, :, :, :, :, 0] = 0
    return {"x": x.reshape(N, 128, 4 * C), "u": u.reshape(N, 128, 512), "v": d["v"], "nb": links_of(rng), **weights(rng, w)}
def setup_inputs_near(rng):
    d = numbers_of(rng)
    x = d["x"].astype(np.float32).reshape(N, 8, 16, C, 4)
    x[:, :, 0] = 0
    x[:, :, 8:] = 0
    s = rng.integers(0, 16, (N, 8, C))
    s = ((s[:, :, :, None] >> np.arange(4)) & 1) * np.exp2(np.arange(4) - 23.0)
    u = d["u"].reshape(N, 128, 128, 4)
    u[:, :, ::16] = 0
    nb = np.stack([some_links(rng) for r in range(N)])
    n = np.arange(C)
    first = n // 3 * 3 % (C - C % 3)
    o = rng.permutation(N) % 4
    for r in range(N):
        k = 1.0 if o[r] == 0 else 2.0 ** -30
        if o[r] < 2:
            x[r, :, 0, :, 0] = rng.choice([-1.0, 1.0], (8, C))
            x[r, :, 11, :, 0] = 2.0 ** -10
            x[r, :, 8] = s[r]
            g, e = rng.integers(8), rng.permutation(C)
            nb[r, g, 0, e], nb[r, g, 1, e] = e[first + (n + 1) % 3], e[first + (n + 2) % 3]
            x[r, g, 0, C - 1, 0] = 1.0
            x[r, g, 8, C - 1] = np.exp2(np.arange(4) - 23.0)
        elif o[r] == 2:
            x[r, :, 8, :, 0] = rng.integers(-1, 3, (8, C)) * 2.0 ** -29
            for g in rng.permutation(8)[:4]: x[r, g, 8, rng.integers(C), 0] = rng.choice([-1.0, 1.0]) * 2.0 ** 29
        else:
            x[r, :, 0, :, 0] = rng.choice([0.0, 0.0, 0.0, 0.0, 0.0, 0.0, 1.0, -1.0], (8, C))
            x[r, :, 8] = s[r] * rng.choice([-1.0, 1.0], (8, C, 1))
        for h in range(0, 128, 16):
            u[r, h, h, 0] = 1.0 if o[r] == 3 else 0.0 if o[r] == 2 else k
            u[r, h + 8, h] = k
            if o[r] < 2: u[r, h + 11, h, 0] = k
    w = layers(rng)
    for i in [0, 8, 9, 10, 11, 12, 13, 14, 15]:
        w[:, :, i] = 0
        w[:, :, :, :, :, i] = 0
    return {"x": x.reshape(N, 128, 4 * C).astype(BF), "u": u.reshape(N, 128, 512), "v": d["v"], "nb": np.stack([gtable(nb[r].reshape(8, 2 * C)) for r in range(N)]), **weights(rng, w)}
def setup_inputs_huge(rng):
    d = numbers_of(rng)
    c = rng.choice([-1.0, 1.0], (N, 1, C, 1))
    c[rng.permutation(N)[:N // 2]] = -1.0
    x = 2.0 ** 30 * (0.6 + 0.2 * rng.random((N, 128, C, 4))) * c
    u = d["u"].reshape(N, 128, 128, 4)
    u[:, :, ::16] = (2.0 ** 30 * (1.0 - 0.1 * rng.random((N, 128, 8, 4)))).astype(np.float32).astype(BF)
    w = np.zeros((N, 128, 4, 128, 4), np.float32)
    i = np.arange(128)
    for b in range(4): w[:, i, b, i, b] = -2
    return {"x": x.astype(np.float32).reshape(N, 128, 4 * C).astype(BF), "u": u.reshape(N, 128, 512), "v": d["v"], "nb": links_of(rng), **weights(rng, w.astype(BF))}
def setup_inputs_forms(rng):
    d = numbers_of(rng)
    x = d["x"].astype(np.float32).reshape(N, 8, 16, C, 4)
    a = (1.0 + (2 * rng.integers(0, 64, (N, 8, 8, C, 4)) + 1) * 2.0 ** -7) * np.exp2(-rng.integers(8, 14, (N, 8, 8, C, 4)).astype(np.float64))
    x[:, :, :8] = a * rng.choice([-1.0, 1.0], a.shape)
    x[:, :, 0, :, 0] = rng.choice([1.875, 1.96875], (N, 8, C))
    x[:, :, 1, :, 0] = rng.integers(8, 10, (N, 8, C)) * rng.choice([-1.0, 1.0], (N, 8, C)) * 2.0 ** -16
    u = d["u"].reshape(N, 128, 128, 4)
    u[:, :, ::16] = 0
    for h in range(0, 128, 16): u[:, h + 1, h, 0] = 1
    nb = np.stack([some_links(rng) for r in range(N)])
    o = rng.permutation(N) % 4
    for r in range(N):
        count = rng.permutation([M, M, M, M - 1, M + 1, 1, 0, C])
        for g in range(8):
            if o[r] == 0: nb[r, g, 1] = nb[r, g, 0]
            if o[r] in (1, 2):
                n = rng.integers(0, 2 * L - 1, C)
                n[:2 * L - 2] = np.arange(1, 2 * L - 1)
                n[2 * L - 2] = 2 * L - 2
                if o[r] == 1: n[L - 2] = 2 * L - 2
                else: n[2 * L - 3] = 0
                m = n.copy()
                e = 2 * L - 1 + np.arange(min(int(count[g]), C - 2 * L + 1))
                if o[r] == 1: n[e] = rng.integers(0, 2, len(e)) * (L - 1)
                else: n[e] = rng.integers(0, 2 * L - 2, len(e))
                m[e] = (n[e] + L - 1) % (2 * L - 2)
                k = rng.permutation(C)
                nb[r, g, 0, k], nb[r, g, 1, k] = k[n], k[m]
    return {"x": x.reshape(N, 128, 4 * C).astype(BF), "u": u.reshape(N, 128, 512), "v": d["v"], "nb": np.stack([gtable(nb[r].reshape(8, 2 * C)) for r in range(N)]), **weights(rng, layers(rng))}
def setup_inputs_spread(rng):
    d = setup_inputs(rng)
    d["x"] = big(wide(rng, N, 128, 4 * C, cols=6))
    return d
def check_inputs(d):
    b = []
    for k in ("x", "u", "v"):
        a = np.abs(d[k].astype(np.float32))
        if not (np.isfinite(a).all() and ((a == 0) | (a >= 2.0 ** -30) & (a <= 2.0 ** 30)).all()): b.append("a value of " + k)
    if not ((d["nb"] >= 0) & (d["nb"] < C)).all(): b.append("an entry of nb")
    none, least, most = [emit(mx_ref.quantize(np.full((128, 16), k, np.float32).astype(BF)))[1][0, 0] for k in (0.0, 2.0 ** -30, 2.0 ** 30)]
    for r in range(N):
        if ((d["wc"][r] == 0x7F) | (d["wc"][r] == 0xFF)).any(): b.append("wc: a code that is no number")
        s = mx_ref.live(d["ws"][r])
        if ((s != none) & ((s < least) | (s > most))).any(): b.append("ws: a scale out of range")
    return b
def bubbles(a, s):
    at = lambda t, e: np.take_along_axis(t, e, axis=1)
    c = np.where(s > 0, a[:, C:], a[:, :C])
    p, q = [a[:, :C]], [a[:, C:]]
    for k in range(1, L):
        p.append(at(c, p[-1]))
        q.append(at(c, q[-1]))
    i, j = np.full((8, C), -1), np.full((8, C), -1)
    for n in reversed(range(2 * L - 1)):
        for k in reversed(range(max(0, n - L + 1), min(n, L - 1) + 1)):
            met = p[k] == q[n - k]
            i[met], j[met] = k, n - k
    is_bubble = (i >= 0) & (p[0] != q[0])
    o = np.lexsort((-s, ~is_bubble))[:, :M]
    filled = at(is_bubble, o)
    g, k = np.arange(8)[:, None, None], np.arange(L)
    np0 = np.stack(p, axis=2)[g, o[:, :, None], np.minimum(k, at(i, o)[:, :, None])]
    nq0 = np.stack(q, axis=2)[g, o[:, :, None], np.minimum(k, at(j, o)[:, :, None])]
    one = at(s, at(q[0], o)) > at(s, at(p[0], o))
    new = a.copy()
    h, m = np.nonzero(filled)
    new[h, (o + C * ~one)[h, m]] = np0[h, m, L - 1]
    slots = [np.where(filled[:, :, None], t, -1).reshape(8, L * M) for t in (np0, nq0, np.where(one[:, :, None], nq0, np0))]
    e = np.full((8, C), -1)
    for n in reversed(range(L * M)):
        h = np.flatnonzero(slots[2][:, n] >= 0)
        e[h, slots[2][h, n]] = n
    return slots[0], slots[1], e, new
def reference(x, u, v, nb, wc, ws):
    qu = [mx_ref.quantize(u[r]) for r in range(N)]
    lay = [pk(wc[r], ws[r]) for r in range(N)]
    now = [x[r] for r in range(N)]
    links = [gentries(nb[r]).astype(np.int64) for r in range(N)]
    for t in range(R):
        own, sent, place = [], [], []
        for r in range(N):
            q = mx_ref.quantize(now[r])
            own.append(decode(q))
            s = mx_ref.matmul(qu[r], q)[::16] + np.float32(0.0)
            a, b, e, links[r] = bubbles(links[r], s)
            place.append(e)
            w = own[r].astype(BF)
            sent.append(mx_ref.quantize(((gcols(w, a).astype(np.float32) + gcols(w, b).astype(np.float32)) * np.float32(0.5)).astype(BF)))
        for r in range(N):
            came, made = sent[(r - 1) % N], []
            for b in range(4):
                h = mx_ref.matmul(pick(lay[r], np.arange(128 * b, 128 * b + 128)), came) * np.float32(0.03125)
                made.append(gpick(np.concatenate([h, np.zeros((128, 1), np.float32)], axis=1), place[r]) + own[r][:, b::4])
            now[r] = tile(made)
    y, ol = np.zeros((N, 128, C), np.float32), np.zeros((N, 8, 2 * C), np.float32)
    oc, osc = np.zeros((N, 128, 4 * C), np.uint8), np.zeros((N, 16, C), np.uint8)
    for r in range(N):
        q = mx_ref.quantize(now[r])
        y[r] = mx_ref.matmul(mx_ref.quantize(v[r]), q)
        ol[r] = links[r]
        oc[r], osc[r] = emit(q)
    return {"y": y, "ol": ol, "oc": oc, "osc": osc}

@@ -1,0 +1,359 @@
+import numpy as np
+from concourse.mybir import dt, AluOpType, ActivationFunctionType, AxisListType
+
+N = 8
+R = 3
+C = 256
+NS = 10
+BIG = 131072.0
+F32, BF, I32, U16, U8, X4 = "float32", "bfloat16", "int32", "uint16", "uint8", "float8_e4m3fn_x4"
+
+
+def _sb(n, d):
+    return ("sbuf", [128, n], d)
+
+
+SCRATCH = {
+    "xt": _sb(1024, BF), "xs": _sb(1024, BF), "ut": _sb(512, BF), "vt": _sb(512, BF), "et": _sb(2048, BF),
+    "eye": _sb(128, BF), "one": _sb(128, BF),
+    "xq": _sb(256, X4), "xp": _sb(256, U8), "uq": _sb(128, X4), "up": _sb(128, U8), "uq2": _sb(128, X4),
+    "up2": _sb(128, U8), "vq": _sb(128, X4), "vp": _sb(128, U8), "eq": _sb(512, X4), "ep": _sb(512, U8),
+    "wq": _sb(512, X4), "wp": _sb(512, U8),
+    "zt": _sb(768, BF), "zq": _sb(192, X4), "zp": _sb(192, U8),
+    "pi": _sb(4, I32), "pf": _sb(16, F32), "idw": _sb(512, F32), "rp": _sb(256, F32), "nmask": _sb(256, F32),
+    "sc0": _sb(256, F32), "nw": _sb(16, F32), "nT": _sb(256, F32), "kk": _sb(192, F32), "rv": _sb(24, F32),
+    "scab": _sb(24, F32), "exl": _sb(16, U16), "upl": _sb(8, U16), "w256": _sb(512, F32), "w1024": _sb(272, F32),
+    "w64": _sb(272, F32), "n64": _sb(16, F32), "nm": _sb(2, F32), "mc": _sb(2, F32), "md": _sb(576, F32),
+    "v0": _sb(256, F32), "a1": _sb(256, F32), "a2": _sb(256, F32), "a3": _sb(256, F32), "a4": _sb(256, F32),
+    "asc": _sb(256, F32), "ct": _sb(8, F32),
+    "ms": _sb(256, F32), "sc": _sb(256, F32), "ssb": _sb(256, F32), "cf": _sb(48, F32),
+    "wc16": _sb(16, U16), "va": _sb(256, F32), "vb": _sb(256, F32), "pq": _sb(784, F32),
+    "t3": ("sbuf", [128, 32, 16], F32), "e3": ("sbuf", [128, 16, 36], BF), "e2": _sb(576, BF), "so": _sb(576, F32),
+    "ne": _sb(16, F32), "hit": _sb(32, F32), "yv": _sb(16, F32), "ex": _sb(256, F32),
+    "ur": _sb(256, F32), "jk": _sb(4096, BF), "acc": _sb(16, F32), "acc2": _sb(16, F32),
+    "a16": _sb(16, U16), "nB": _sb(32, F32), "kap": _sb(256, F32), "r16": _sb(16, U16),
+    "qq": _sb(256, F32), "xk0": _sb(264, F32), "xk1": _sb(264, F32), "kv": _sb(2, F32), "kq": _sb(2, I32),
+    "kn": _sb(2, I32), "off": _sb(8, U16), "g2": _sb(128, F32), "t2": ("sbuf", [128, 8, 16], F32),
+    "w2": ("sbuf", [128, 4, 20], F32), "ij": _sb(8, I32), "ijf": _sb(4, F32),
+    "ff": ("sbuf", [128, 4, 6], F32), "dd": ("sbuf", [128, 4, 6], F32), "d2": _sb(24, F32), "ab": _sb(24, F32),
+    "ab16": _sb(24, U16), "br": _sb(2, F32), "dba": _sb(12, F32), "bt": _sb(12, F32), "bt16": _sb(12, U16),
+    "ke": _sb(192, F32), "abd": _sb(3200, F32), "ev": _sb(16, F32), "ei": _sb(64, I32), "e16": _sb(16, U16),
+    "li": _sb(20, I32), "ln16": _sb(2, U16), "mt": _sb(32, I32), "lt": _sb(560, I32), "lw": _sb(32, I32),
+    "lw16": _sb(32, U16), "dl": _sb(16, F32), "olr": _sb(512, F32), "ysb": _sb(256, F32),
+    "at": _sb(768, BF), "f2": _sb(1088, BF), "fw": _sb(1024, BF), "hb": _sb(896, F32),
+}
+for _t in range(R):
+    SCRATCH["yq%d" % _t] = _sb(192, X4)
+    SCRATCH["yp%d" % _t] = _sb(192, U8)
+PS = ["ps1", "ps2", "pd0", "pd1", "pd2", "pd3", "ph0", "ph1"]
+for _n in PS:
+    SCRATCH[_n] = ("psum", [128, 512], F32)
+
+DMAS = ["dx", "du", "dv", "dwc", "dws", "dn0", "dn1", "dlt", "das", "dl0", "dl1", "oy", "ool", "ooc", "os0", "os1", "os2", "os3"]
+SEMAPHORES = ["sv", "ss", "sp", "sg", "lc"] + ["ar%d" % t for t in range(R)] + DMAS
+
+
+def rank_program(g, core, T, topo):
+    rank = T.rank_of(core)
+    if rank is None:
+        return
+    A = AluOpType
+    ACT = ActivationFunctionType
+    XAX = AxisListType.X
+    queues = {"v": g.vector, "s": g.scalar, "p": g.tensor, "g": g, "y": g.sync}
+    total, waited, wr, rd = {}, {q: {} for q in queues}, {}, {}
+
+    def need(q, deps):
+        best = {}
+        for s, n in deps:
+            best[s] = max(best.get(s, 0), n)
+        for s in sorted(best):
+            if waited[q].get(s, 0) < best[s]:
+                queues[q].wait_ge(T.sem[s], best[s])
+                waited[q][s] = best[s]
+
+    def before(q, reads, writes):
+        deps = []
+        for k in reads:
+            if k in wr:
+                deps.append(wr[k][1:])
+            if k in PS:
+                deps += [r[1:] for r in rd.get(k, []) if r[0] != q]
+        for k in writes:
+            if k in wr:
+                deps.append(wr[k][1:])
+            deps += [r[1:] for r in rd.get(k, [])]
+        need(q, deps)
+
+    def after(q, sem, inc, reads, writes):
+        total[sem] = total.get(sem, 0) + inc
+        tok = (q, sem, total[sem])
+        for k in writes:
+            wr[k] = tok
+            rd[k] = []
+        for k in reads:
+            if k not in writes:
+                rd[k] = [r for r in rd.get(k, []) if r[1] != sem] + [tok]
+
+    def op(q, reads, writes, name, *args, **kw):
+        before(q, reads, writes)
+        fns = {"memset": g.vector.memset, "tt": g.vector.tensor_tensor, "ts": g.vector.tensor_scalar,
+               "cp": g.vector.tensor_copy, "red": g.vector.tensor_reduce, "scan": g.vector.tensor_tensor_scan,
+               "tr": g.vector.transpose, "qz": g.vector.quantize_mx, "act": g.scalar.activation,
+               "mm": g.tensor.matmul_mx, "iota": g.iota, "asel": g.affine_select}
+        fns[name](*args, **kw).then_inc(T.sem["s" + q], 1)
+        after(q, "s" + q, 1, reads, writes)
+
+    def dma(q, sem, reads, writes, out, in_):
+        before(q, reads, writes)
+        queues[q].dma_start(out, in_).then_inc(T.sem[sem], 16)
+        after(q, sem, 16, reads, writes)
+
+    def V(name, writes, reads, *args, **kw):
+        op("v", reads.split(), writes.split(), name, *args, **kw)
+
+    def S(writes, reads, out, in_, func, **kw):
+        op("s", reads.split(), writes.split(), "act", out, in_, func, **kw)
+
+    dma("y", "dx", [], ["xt"], T.xt[:], T.x[:])
+    dma("s", "du", [], ["ut"], T.ut[:], T.u[:])
+    dma("y", "dn0", [], ["lw", "lwb"], T.lw[:], T.nb[:])
+    dma("s", "dwc", [], ["wq"], T.wq[:, 0:512].bitcast(dt.uint8), T.wc[:])
+    dma("y", "dn1", [], ["lt0"], T.lt[0:128:16, 0:256], T.nb[:, 0:16])
+    dma("y", "dlt", [], ["lt1"], T.lt[0:128:16, 256:512], T.nb[:, 16:32])
+    dma("s", "dws", [], ["wp"], T.wp[:, 0:512], T.ws[:])
+    dma("y", "dv", [], ["vt"], T.vt[:], T.v[:])
+
+    def iota(key, out, pattern, base, cm):
+        kw = {} if key == "pi" else {"allow_small_or_imprecise_dtypes": True}
+        op("g", [], [key], "iota", out, pattern, base, cm, **kw)
+    V("memset", "one", "", T.one[:], 1.0)
+    V("memset", "et", "", T.et[:], 0.0)
+    op("g", ["one"], ["eye"], "asel", T.eye[:], T.one[:], [[-1, 128]], A.is_equal, 0.0, 0, 1)
+    iota("pi", T.pi[:, 0:1], [[0, 1]], 0, 1)
+    iota("rp", T.rp[:], [[0, 16], [1, 16]], 0, 0)
+    iota("idw", T.idw[:], [[1, 512]], 0, 0)
+    iota("nw", T.nw[:], [[16, 16]], 0, 0)
+    iota("nT", T.nT[:], [[32, 8], [0, 32]], 1, 0)
+    iota("kk", T.kk[:], [[1, 6], [8, 32]], 0, 0)
+    iota("rv", T.rv[:], [[0, 4], [1, 6]], 0, 0)
+    for b in range(4):
+        V("cp", "et", "eye", T.et[:, 512 * b + b:512 * b + 512:4], T.eye[:])
+    V("qz", "eq ep", "et", T.eq[:, 0:512], T.ep[:, 0:512], T.et[:, 0:2048])
+    V("qz", "xq xp", "xt", T.xq[:, 0:256], T.xp[:, 0:256], T.xt[:, 0:1024])
+    V("qz", "uq up", "ut", T.uq[:, 0:128], T.up[:, 0:128], T.ut[:, 0:512])
+    V("ts", "upl", "idw", T.upl[:], T.idw[:, 0:8], 16.0, None, A.mult)
+    V("cp", "uq2", "uq upl", T.uq2[:, 0:128].bitcast(dt.uint32), T.uq[:, 0:128].bitcast(dt.uint32).indirect(T.upl[:, 0:8]))
+    V("cp", "up2", "up upl", T.up2[:, 0:128], T.up[:, 0:128].indirect(T.upl[:, 0:8]))
+    V("ts", "pi1", "pi", T.pi[:, 1:2], T.pi[:, 0:1], 15, None, A.bitwise_and)
+    V("ts", "pi2", "pi", T.pi[:, 2:3], T.pi[:, 0:1], 31, None, A.bitwise_and)
+    V("ts", "pi3", "pi", T.pi[:, 3:4], T.pi[:, 0:1], 4, 1, A.arith_shift_right, A.bitwise_and)
+    V("cp", "pf", "pi1 pi2 pi3", T.pf[:, 0:3], T.pi[:, 1:4])
+    V("ts", "pf3", "pf", T.pf[:, 3:4], T.pf[:, 2:3], -1.0, 1.0, A.mult, A.add)
+    r16, p32 = T.pf[:, 0:1], T.pf[:, 1:2]
+    V("ts", "nmask", "rp pf", T.nmask[:], T.rp[:], r16, -1.0, A.is_equal, A.mult)
+    V("ts", "sc0", "rp", T.sc0[:], T.rp[:], 0.0, None, A.not_equal)
+    V("ts", "nw", "nw pf", T.nw[:], T.nw[:], r16, None, A.add)
+    V("ts", "nT", "nT pf", T.nT[:], T.nT[:], p32, None, A.add)
+    V("ts", "kk", "kk", T.kk[:], T.kk[:], 0.125, None, A.mult)
+    V("ts", "scab", "rv", T.scab[:], T.rv[:], 0.0, None, A.not_equal)
+    V("cp", "exl", "idw", T.exl[:], T.idw[:, 0:16])
+    V("ts", "w256", "idw", T.w256[:], T.idw[:], 256.0, -65280.0, A.mult, A.add)
+    V("ts", "w1024", "idw", T.w1024[:], T.idw[:, 0:272], 1024.0, BIG, A.mult, A.min)
+    V("ts", "w64", "idw", T.w64[:], T.idw[:, 0:272], 64.0, None, A.mult)
+    V("ts", "n64", "nw", T.n64[:], T.nw[:], -64.0, None, A.mult)
+    for b in range(2):
+        V("ts", "nm%d" % b, "pf", T.nm[:, b:b + 1], r16, -1024.0, -16384.0 * b, A.mult, A.add)
+        V("ts", "mc%d" % b, "pf", T.mc[:, b:b + 1], r16, 224.0 + 16.0 * b, None, A.add)
+    for t, k in enumerate(["v0", "a1", "a2", "a3", "a4", "asc"]):
+        V("ts", "ra", "pf", T.ct[:, 4:5], r16, float(5 - t), None, A.is_equal)
+        V("ts", "rb", "pf", T.ct[:, 5:6], r16, float(8 + t), None, A.is_equal)
+        V("tt", "rb", "ra rb", T.ct[:, 5:6], T.ct[:, 4:5], T.ct[:, 5:6], A.add)
+        V("ts", k, "idw rb", T[k][:], T.idw[:, 0:256], T.ct[:, 5:6], None, A.mult)
+    for kind in range(2):
+        for hh in range(2):
+            e = T.pf[:, 3 - hh:4 - hh]
+            V("ts", "ct%d" % (2 * kind + hh), "pf pf3", T.ct[:, 2 * kind + hh:2 * kind + hh + 1], e, 256.0 * kind - 513.0, 513.0, A.mult, A.add)
+    pairs = [(i, s - i) for s in range(10, 0, -1) for i in range(min(5, s), max(0, s - 5) - 1, -1)]
+    worth = [8 * (i + j) + i for i, j in pairs] + [0]
+    V("memset", "md", "", T.md[:], -1.0 / 128)
+    V("memset", "md", "", T.md[:, 0:576:36], -4.0)
+    for k in range(len(pairs)):
+        d = worth[k] - worth[k + 1]
+        if d != 1:
+            V("memset", "md", "", T.md[:, k + 1:576:36], -d / 128.0)
+    V("memset", "e3", "", T.e3[:, :, 0], 0.0)
+    V("memset", "pq", "", T.pq[:, 512:784], 0.0)
+    V("memset", "pq", "", T.pq[:, 512:513], 256.0)
+    V("memset", "pq", "", T.pq[:, 768:769], 256.0)
+    V("memset", "xk0", "", T.xk0[:, 256:264], 512.0)
+    V("memset", "xk1", "", T.xk1[:, 256:264], 512.0)
+    V("memset", "w2z", "", T.w2[:, :, 0], 0.0)
+    V("memset", "f2z", "", T.f2[:], 0.0)
+    V("memset", "hbz", "", T.hb[:], 0.0)
+    for c in range(16):
+        V("memset", "abz", "", T.abd[:, 200 * c + 192:200 * c + 200], 31.75)
+    V("qz", "vq vp", "vt", T.vq[:, 0:128], T.vp[:, 0:128], T.vt[:, 0:512])
+
+    def lists():
+        V("cp", "lw16", "lw lwb", T.lw16[:], T.lw[:])
+        V("tt", "dl", "lw lwb", T.dl[:], T.lw[:, 16:32], T.lw[:, 0:16], A.subtract)
+    lists()
+
+    def mm(out, st, stk, sc, mv, mvk, mp, n):
+        op("p", stk.split() + mvk.split(), [out], "mm", T[out][:, 0:n], st, sc, mv, mp, True, True)
+
+    dst = T.cores[(rank + 1) % N]
+    prv = T.cores[(rank - 1) % N]
+
+    def engs(a, b):
+        e = topo.engines(a, b)
+        return e[::len(e) // 8]
+    emask = sum(1 << k for k in engs(core, dst))
+    rid, pid = topo.addr(dst)[:2]
+
+    def send(t):
+        before("g", ["zq", "zp"], [])
+        n = len(engs(core, dst))
+        g.remote_dma(T["yq%d" % t][:, 0:192].bitcast(dt.uint8), T.zq[:, 0:192].bitcast(dt.uint8), T.sem["ar%d" % t], T.sem.lc, pid, rid, emask)
+        g.remote_dma(T["yp%d" % t][:, 0:192], T.zp[:, 0:192], T.sem["ar%d" % t], T.sem.lc, pid, rid, emask)
+        after("g", "lc", 2 * n, ["zq", "zp"], [])
+        m = 2 * len(engs(prv, core))
+        total["ar%d" % t] = m
+        wr["y%d" % t] = ("r", "ar%d" % t, m)
+
+    for t in range(R):
+        xq, xp = T.xq[:, 0:256], T.xp[:, 0:256]
+        for k in ("ps1", "ps2"):
+            mm(k, T.uq2[:, 0:128], "uq2 up2", T.up2[:, 0:128], xq, "xq xp", xp, 256)
+        for b in range(4):
+            mm("pd%d" % b, T.eq[:, 128 * b:128 * b + 128], "eq ep", T.ep[:, 128 * b:128 * b + 128], xq, "xq xp", xp, 256)
+        V("tt", "ms", "ps1 nmask", T.ms[:], T.ps1[:, 0:256], T.nmask[:], A.mult)
+        S("ssb", "ps2", T.ssb[:], T.ps2[:, 0:256], ACT.Copy)
+        dma("y", "das", ["ssb"], ["asc"], T.asc[15:128:16, :], T.ssb[15:128:16, :])
+        V("scan", "sc", "ms sc0", T.sc[:], T.sc0[:], T.ms[:], 0.0, A.mult, A.add)
+        V("ts", "cf", "sc", T.cf[:, 0:16], T.sc[:, 15:256:16], 0.0, None, A.is_lt)
+        V("tt", "c1", "cf dl", T.cf[:, 16:32], T.cf[:, 0:16], T.dl[:], A.mult)
+        V("tt", "c2", "c1 lw lwb", T.cf[:, 32:48], T.cf[:, 16:32], T.lw[:, 0:16], A.add)
+        V("cp", "wc16", "c2", T.wc16[:], T.cf[:, 32:48])
+        for c in range(16):
+            S("jk%d acc%d" % (c, c), "ssb sc", T.jk[:, 256 * c:256 * c + 256], T.ssb[:], ACT.Sign, bias=T.sc[:, 16 * c + 15:16 * c + 16], scale=1.0, accum_out=T.acc[:, c:c + 1])
+        cur = "v0"
+        for k, add in enumerate(["a1", "a2", "a3", "a4", "asc"]):
+            nxt = "va" if k % 2 == 0 else "vb"
+            V("tt", nxt, cur + " wc16 " + add, T[nxt][:], T[cur][:, 0:256].indirect(T.wc16[:, 0:16]), T[add][:], A.add)
+            cur = nxt
+        V("cp", "pq0", cur + " lw16 pq", T.pq[:, 0:256], T[cur][:, 0:256].indirect(T.lw16[:, 0:16]))
+        V("cp", "pq1", cur + " lw16 pq", T.pq[:, 256:512], T[cur][:, 0:256].indirect(T.lw16[:, 16:32]))
+        V("tr", "t3", "pq0 pq1", T.t3[:], T.pq[:, 0:512])
+        k = 1
+        for s in range(10, 0, -1):
+            hi, lo = min(5, s), max(0, s - 5)
+            n = hi - lo + 1
+            V("tt", "e3_%d" % s, "t3 e3", T.e3[:, :, k:k + n], T.t3[:, 0:16, 13 - hi:14 - lo], T.t3[:, 16:32, s - hi:s - lo + 1], A.is_equal)
+            k += n
+        V("tt", "ne", "t3", T.ne[:], T.t3[:, 0:16, 0], T.t3[:, 16:32, 0], A.not_equal)
+        V("cp", "e2", "e3 " + " ".join("e3_%d" % s for s in range(1, 11)), T.e2[:], T.e3[:])
+        V("scan", "so", "e2 md", T.so[:], T.e2[:], T.md[:], 0.0, A.max, A.add)
+        V("tt", "hit", "so ne", T.hit[:, 0:16], T.so[:, 35:576:36], T.ne[:], A.mult)
+        V("ts", "hy", "hit", T.hit[:, 16:32], T.hit[:, 0:16], 0.0, BIG, A.is_le, A.mult)
+        V("tt", "yv", "hy hit", T.yv[:], T.hit[:, 16:32], T.hit[:, 0:16], A.subtract)
+        V("tt", "ex", "yv exl nT", T.ex[:], T.yv[:, 0:16].indirect(T.exl[:, 0:16]), T.nT[:], A.add)
+        V("tr", "ur", "ex", T.ur[:], T.ex[:])
+        accs = " ".join("acc%d" % c for c in range(16))
+        V("ts", "a16", accs, T.a16[:], T.acc[:], 255.0, None, A.add)
+        V("ts", "nb0", accs, T.nB[:, 16:32], T.acc[:], -256.0, None, A.mult)
+        V("tt", "kap", "a16 w256 ur", T.kap[:], T.w256[:, 0:512].indirect(T.a16[:, 0:16]), T.ur[:], A.add)
+        V("tt", "nB", "nb0 nw", T.nB[:, 0:16], T.nB[:, 16:32], T.nw[:], A.subtract)
+        for c in range(NS):
+            S("jk%d rk%d" % (c, c), "kap nB", T.jk[:, 256 * c:256 * c + 256], T.kap[:], ACT.Sign, bias=T.nB[:, c:c + 1], scale=1.0, accum_out=T.acc2[:, c:c + 1])
+        for c in range(NS, 16):
+            V("ts", "jk%d" % c, "kap nB", T.jk[:, 256 * c:256 * c + 256], T.kap[:], T.nB[:, c:c + 1], 0.0, A.add, A.is_lt)
+        for c in range(NS, 16):
+            V("red", "rk%d" % c, "jk%d" % c, T.acc2[:, c:c + 1], T.jk[:, 256 * c:256 * c + 256], XAX, A.add)
+        V("cp", "r16b", " ".join("rk%d" % c for c in range(NS, 16)), T.r16[:, NS:16], T.acc2[:, NS:16])
+        V("ts", "r16a", " ".join("rk%d" % c for c in range(NS)), T.r16[:, 0:NS], T.acc2[:, 0:NS], -0.5, 128.0, A.mult, A.add)
+        V("tt", "qq", "r16a r16b w1024 ur", T.qq[:], T.w1024[:, 0:272].indirect(T.r16[:, 0:16]), T.ur[:], A.add)
+        S("xk1a", "qq nm1", T.xk1[:, 0:256], T.qq[:], ACT.Identity, bias=T.nm[:, 1:2], scale=1.0)
+        V("ts", "xk0a", "qq nm0", T.xk0[:, 0:256], T.qq[:], T.nm[:, 0:1], None, A.add)
+        V("red", "kv0", "xk0 xk0a", T.kv[:, 0:1], T.xk0[:, 0:264], XAX, A.min, apply_absolute_value=True)
+        V("red", "kv1", "xk1 xk1a", T.kv[:, 1:2], T.xk1[:, 0:264], XAX, A.min, apply_absolute_value=True)
+        for b in range(4):
+            S("f2_%d" % b, "pd%d f2z" % b, T.f2[:, 272 * b:272 * b + 256], T["pd%d" % b][:, 0:256], ACT.Copy, scale=0.5)
+        V("ts", "kq", "kv0 kv1", T.kq[:], T.kv[:], 128.0, None, A.mult)
+        V("ts", "kn", "kq", T.kn[:], T.kq[:], 7, None, A.arith_shift_right)
+        V("ts", "ij0", "kq", T.ij[:, 0:2], T.kq[:], 7, None, A.bitwise_and)
+        V("ts", "sij", "kq", T.ij[:, 4:6], T.kq[:], 3, 15, A.arith_shift_right, A.bitwise_and)
+        for kind in range(2):
+            for hh in range(2):
+                o = 4 * kind + hh
+                c = 2 * kind + hh
+                V("ts", "off%d" % o, "kn pf pf3 ct%d" % c, T.off[:, o:o + 3:2], T.kn[:], T.pf[:, 3 - hh:4 - hh], T.ct[:, c:c + 1], A.mult, A.add)
+        V("cp", "g2", "pq pq0 pq1 off0 off1 off4 off5", T.g2[:], T.pq[:, 0:784].indirect(T.off[:, 0:8]))
+        V("tt", "ij1", "sij ij0", T.ij[:, 2:4], T.ij[:, 4:6], T.ij[:, 0:2], A.subtract)
+        V("tr", "t2", "g2", T.t2[:], T.g2[:])
+        V("cp", "ijf", "ij0 ij1", T.ijf[:], T.ij[:, 0:4])
+        V("tt", "w2", "t2", T.w2[:, :, 1:17], T.t2[:, 0:8:2, :], T.t2[:, 1:8:2, :], A.add)
+        for b in range(4):
+            V("ts", "ff%d" % b, "rv ijf", T.ff[:, b, :], T.rv[:, 0:6], T.ijf[:, b:b + 1], None, A.is_le)
+        V("tt", "dd", "w2 w2z", T.dd[:], T.w2[:, :, 1:7], T.w2[:, :, 0:6], A.subtract)
+        V("tt", "d2", "dd ff0 ff1 ff2 ff3", T.d2[:], T.dd[:], T.ff[:], A.mult)
+        V("scan", "ab", "d2 scab", T.ab[:], T.scab[:], T.d2[:], 0.0, A.mult, A.add)
+        for kind in range(2):
+            for b in range(2):
+                o = 12 * kind
+                V("cp", "ab16_%d%d" % (kind, b), "ab", T.ab16[:, o + b:o + 12:2], T.ab[:, o + 6 * b:o + 6 * b + 6])
+        for b in range(4):
+            S("at%d" % b, "f2z f2_%d ab16_00 ab16_01" % b, T.at[:, 192 * b:192 * b + 192], T.f2[:, 272 * b:272 * b + 272].indirect(T.ab16[:, 0:12]), ACT.Copy)
+            V("tt", "zt%d" % b, "f2z f2_%d ab16_10 ab16_11 at%d" % (b, b), T.zt[:, b:768:4], T.f2[:, 272 * b:272 * b + 272].indirect(T.ab16[:, 12:24]), T.at[:, 192 * b:192 * b + 192], A.add)
+        V("qz", "zq zp", "zt0 zt1 zt2 zt3", T.zq[:, 0:192], T.zp[:, 0:192], T.zt[:, 0:768])
+        send(t)
+        V("tt", "br", "w2", T.br[:], T.w2[:, 2:4, 16], T.w2[:, 0:2, 16], A.is_gt)
+        V("tt", "dba", "ab", T.dba[:], T.ab[:, 12:24], T.ab[:, 0:12], A.subtract)
+        for b in range(2):
+            V("ts", "bt_%d" % b, "dba br", T.bt[:, 6 * b:6 * b + 6], T.dba[:, 6 * b:6 * b + 6], T.br[:, b:b + 1], None, A.mult)
+        V("tt", "dba", "bt_0 bt_1 ab", T.dba[:], T.bt[:], T.ab[:, 0:12], A.add)
+        for b in range(2):
+            V("cp", "bt16_%d" % b, "dba", T.bt16[:, b:12:2], T.dba[:, 6 * b:6 * b + 6])
+        V("tt", "ke", "bt16_0 bt16_1 w64 kk", T.ke[:], T.w64[:, 0:272].indirect(T.bt16[:, 0:12]), T.kk[:], A.add)
+        for b in range(4):
+            S("fw%d" % b, "pd%d" % b, T.fw[:, 256 * b:256 * b + 256], T["pd%d" % b][:, 0:256], ACT.Copy)
+        for c in range(16):
+            S("abd%d" % c, "ke n64 abz", T.abd[:, 200 * c:200 * c + 192], T.ke[:], ACT.Abs, bias=T.n64[:, c:c + 1], scale=1.0)
+        V("ts", "li0", "kn", T.li[:, 0:2], T.kn[:], 15, None, A.bitwise_and)
+        V("ts", "li1", "kn", T.li[:, 2:4], T.kn[:], 4, None, A.arith_shift_right)
+        V("ts", "li2", "kn", T.li[:, 4:6], T.kn[:], 9, None, A.arith_shift_right)
+        V("ts", "li3", "li0", T.li[:, 6:8], T.li[:, 0:2], 16.0, 256.0, A.mult, A.add)
+        V("ts", "li4", "br", T.li[:, 8:10], T.br[:], -256.0, None, A.mult)
+        V("tt", "li5", "li2 mc0 mc1", T.li[:, 10:12], T.li[:, 4:6], T.mc[:], A.mult)
+        V("tt", "li6", "li3 li1", T.li[:, 12:14], T.li[:, 6:8], T.li[:, 2:4], A.add)
+        V("tt", "li7", "li4 li5", T.li[:, 14:16], T.li[:, 8:10], T.li[:, 10:12], A.add)
+        V("tt", "li8", "li6 li7", T.li[:, 16:18], T.li[:, 12:14], T.li[:, 14:16], A.add)
+        V("cp", "mt", "idw ab16_00 ab16_01", T.mt[:], T.idw[:, 0:272].indirect(T.ab16[:, 10:12]))
+        V("cp", "ln16", "li8", T.ln16[:], T.li[:, 16:18])
+        V("cp", "lt0 lt1", "mt ln16", T.lt[:, 0:560].indirect(T.ln16[:, 0:2]), T.mt[:])
+        dma("y", "dl0", ["lt0"], ["lw"], T.lw[:, 0:16], T.lt[0:128:16, 0:256])
+        dma("y", "dl1", ["lt1"], ["lwb"], T.lw[:, 16:32], T.lt[0:128:16, 256:512])
+        for c in range(16):
+            V("red", "ev%d" % c, "abz abd%d" % c, T.ev[:, c:c + 1], T.abd[:, 200 * c:200 * c + 193], XAX, A.min)
+        V("ts", "ei", " ".join("ev%d" % c for c in range(16)), T.ei[:, 0:16], T.ev[:], 256.0, None, A.mult)
+        V("ts", "ek", "ei", T.ei[:, 16:32], T.ei[:, 0:16], 255, None, A.bitwise_and)
+        V("ts", "em", "ei", T.ei[:, 32:48], T.ei[:, 0:16], 8, None, A.arith_shift_right)
+        V("tt", "ex2", "ek em", T.ei[:, 48:64], T.ei[:, 16:32], T.ei[:, 32:48], A.add)
+        V("cp", "e16", "ex2", T.e16[:], T.ei[:, 48:64])
+        ph = ["ph0", "ph1", "ps1", "ps2"]
+        for b in range(4):
+            mm(ph[b], T.wq[:, 128 * b:128 * b + 128], "wq wp", T.wp[:, 128 * b:128 * b + 128], T["yq%d" % t][:, 0:192], "y%d" % t, T["yp%d" % t][:, 0:192], 192)
+            S("hb%d" % b, ph[b] + " hbz", T.hb[:, 224 * b:224 * b + 192], T[ph[b]][:, 0:192], ACT.Copy, scale=0.03125)
+            V("tt", "xs%d" % b, "hbz hb%d e16 fw%d" % (b, b), T.xs[:, b:1024:4], T.hb[:, 224 * b:224 * b + 224].indirect(T.e16[:, 0:16]), T.fw[:, 256 * b:256 * b + 256], A.add)
+        V("qz", "xq xp", "xs0 xs1 xs2 xs3", T.xq[:, 0:256], T.xp[:, 0:256], T.xs[:, 0:1024])
+        lists()
+    dma("y", "ooc", ["xq"], [], T.oc[:, 0:1024], T.xq[:, 0:256].bitcast(dt.uint8))
+    for k in range(4):
+        dma("y" if k % 2 else "s", "os%d" % k, ["xp"], [], T.osc[4 * k:4 * k + 4, 0:256], T.xp[32 * k:32 * k + 4, 0:256])
+    mm("ps1", T.vq[:, 0:128], "vq vp", T.vp[:, 0:128], T.xq[:, 0:256], "xq xp", T.xp[:, 0:256], 256)
+    S("ysb", "ps1", T.ysb[:], T.ps1[:, 0:256], ACT.Copy)
+    dma("s", "oy", ["ysb"], [], T.y[:], T.ysb[:])
+    V("cp", "olr", "idw lw16", T.olr[:], T.idw[:, 0:256].indirect(T.lw16[:, 0:32]))
+    dma("y", "ool", ["olr"], [], T.ol[:], T.olr[0:128:16, :])
+    need("g", [(s, n) for s, n in total.items()])

@@ -20,16 +20,16 @@ SCRATCH = {
     "up2": _sb(128, U8), "vq": _sb(128, X4), "vp": _sb(128, U8), "eq": _sb(512, X4), "ep": _sb(512, U8),
     "wq": _sb(512, X4), "wp": _sb(512, U8),
     "zt": _sb(768, BF), "zq": _sb(192, X4), "zp": _sb(192, U8),
-    "pi": _sb(4, I32), "pf": _sb(16, F32), "idw": _sb(512, F32), "rp": _sb(256, F32), "nmask": _sb(256, F32),
-    "sc0": _sb(256, F32), "nw": _sb(16, F32), "nT": _sb(256, F32), "kk": _sb(192, F32), "rv": _sb(24, F32),
+    "pi": _sb(4, I32), "pf": _sb(4, F32), "sm": _sb(64, F32), "idw": _sb(512, F32), "rp": _sb(256, F32), "nmask": _sb(256, F32),
+    "sc0": _sb(256, F32), "nw": _sb(16, F32), "nT": _sb(256, F32), "nTi": _sb(256, F32), "kk": _sb(192, F32), "rv": _sb(24, F32),
     "scab": _sb(24, F32), "exl": _sb(16, U16), "upl": _sb(8, U16), "w256": _sb(512, F32), "w1024": _sb(272, F32),
     "w64": _sb(272, F32), "n64": _sb(16, F32), "nm": _sb(2, F32), "mc": _sb(2, F32), "md": _sb(576, F32),
     "v0": _sb(256, F32), "a1": _sb(256, F32), "a2": _sb(256, F32), "a3": _sb(256, F32), "a4": _sb(256, F32),
-    "asc": _sb(256, F32), "ct": _sb(8, F32),
+    "asc": _sb(256, F32), "ct": _sb(4, F32),
     "ms": _sb(256, F32), "sc": _sb(256, F32), "ssb": _sb(256, F32), "cf": _sb(48, F32),
     "wc16": _sb(16, U16), "va": _sb(256, F32), "vb": _sb(256, F32), "pq": _sb(784, F32),
     "t3": ("sbuf", [128, 32, 16], F32), "e3": ("sbuf", [128, 16, 36], BF), "e2": _sb(576, BF), "so": _sb(576, F32),
-    "ne": _sb(16, F32), "hit": _sb(32, F32), "yv": _sb(16, F32), "ex": _sb(256, F32),
+    "ne": _sb(32, F32), "yv": _sb(16, F32), "ex": _sb(256, F32),
     "ur": _sb(256, F32), "jk": _sb(4096, BF), "acc": _sb(16, F32), "acc2": _sb(16, F32),
     "a16": _sb(16, U16), "nB": _sb(32, F32), "kap": _sb(256, F32), "r16": _sb(16, U16),
     "qq": _sb(256, F32), "xk0": _sb(264, F32), "xk1": _sb(264, F32), "kv": _sb(2, F32), "kq": _sb(2, I32),
@@ -37,7 +37,7 @@ SCRATCH = {
     "w2": ("sbuf", [128, 4, 20], F32), "ij": _sb(8, I32), "ijf": _sb(4, F32),
     "ff": ("sbuf", [128, 4, 6], F32), "dd": ("sbuf", [128, 4, 6], F32), "d2": _sb(24, F32), "ab": _sb(24, F32),
     "ab16": _sb(24, U16), "br": _sb(2, F32), "dba": _sb(12, F32), "bt": _sb(12, F32), "bt16": _sb(12, U16),
-    "ke": _sb(192, F32), "abd": _sb(3200, F32), "ev": _sb(16, F32), "ei": _sb(64, I32), "e16": _sb(16, U16),
+    "ke": _sb(192, F32), "abd": ("sbuf", [128, 16, 200], F32), "ev": _sb(16, F32), "ei": _sb(64, I32), "e16": _sb(16, U16),
     "li": _sb(20, I32), "ln16": _sb(2, U16), "mt": _sb(32, I32), "lt": _sb(560, I32), "lw": _sb(32, I32),
     "lw16": _sb(32, U16), "dl": _sb(16, F32), "olr": _sb(512, F32), "ysb": _sb(256, F32),
     "at": _sb(768, BF), "f2": _sb(1088, BF), "fw": _sb(1024, BF), "hb": _sb(896, F32),
@@ -118,82 +118,71 @@ def rank_program(g, core, T, topo):
     dma("y", "dx", [], ["xt"], T.xt[:], T.x[:])
     dma("s", "du", [], ["ut"], T.ut[:], T.u[:])
     dma("y", "dn0", [], ["lw", "lwb"], T.lw[:], T.nb[:])
-    dma("s", "dwc", [], ["wq"], T.wq[:, 0:512].bitcast(dt.uint8), T.wc[:])
     dma("y", "dn1", [], ["lt0"], T.lt[0:128:16, 0:256], T.nb[:, 0:16])
     dma("y", "dlt", [], ["lt1"], T.lt[0:128:16, 256:512], T.nb[:, 16:32])
-    dma("s", "dws", [], ["wp"], T.wp[:, 0:512], T.ws[:])
+    dma("y", "dwc", [], ["wq"], T.wq[:, 0:512].bitcast(dt.uint8), T.wc[:])
+    dma("y", "dws", [], ["wp"], T.wp[:, 0:512], T.ws[:])
     dma("y", "dv", [], ["vt"], T.vt[:], T.v[:])
 
-    def iota(key, out, pattern, base, cm):
+    def iota(key, out, pattern, base, cm=0):
         kw = {} if key == "pi" else {"allow_small_or_imprecise_dtypes": True}
         op("g", [], [key], "iota", out, pattern, base, cm, **kw)
     V("memset", "one", "", T.one[:], 1.0)
     V("memset", "et", "", T.et[:], 0.0)
-    op("g", ["one"], ["eye"], "asel", T.eye[:], T.one[:], [[-1, 128]], A.is_equal, 0.0, 0, 1)
     iota("pi", T.pi[:, 0:1], [[0, 1]], 0, 1)
-    iota("rp", T.rp[:], [[0, 16], [1, 16]], 0, 0)
-    iota("idw", T.idw[:], [[1, 512]], 0, 0)
-    iota("nw", T.nw[:], [[16, 16]], 0, 0)
-    iota("nT", T.nT[:], [[32, 8], [0, 32]], 1, 0)
-    iota("kk", T.kk[:], [[1, 6], [8, 32]], 0, 0)
-    iota("rv", T.rv[:], [[0, 4], [1, 6]], 0, 0)
+    iota("sm1", T.sm[:, 8:14], [[-1, 6]], 5)
+    iota("sm2", T.sm[:, 16:22], [[1, 6]], 8)
+    iota("sm0", T.sm[:, 0:8], [[16, 8]], 0)
+    op("g", ["one"], ["eye"], "asel", T.eye[:], T.one[:], [[-1, 128]], A.is_equal, 0.0, 0, 1)
+    iota("idw", T.idw[:], [[1, 512]], 0)
+    iota("rp", T.rp[:], [[0, 16], [1, 16]], 0)
+    iota("sm3", T.sm[:, 24:26], [[16, 2]], 0)
+    iota("rv", T.rv[:], [[0, 4], [1, 6]], 0)
+    iota("nw0", T.sm[:, 32:48], [[16, 16]], 0)
+    iota("exl0", T.sm[:, 48:64], [[1, 16]], 0)
+    iota("pq", T.pq[:, 512:784], [[0, 272]], 0)
+    iota("pq", T.pq[:, 512:513], [[0, 1]], 256)
+    iota("pq", T.pq[:, 768:769], [[0, 1]], 256)
+    pairs = [(i, s - i) for s in range(10, 0, -1) for i in range(min(5, s), max(0, s - 5) - 1, -1)]
+    worth = [8 * (i + j) + i for i, j in pairs] + [0]
+    iota("md", T.md[:], [[0, 576]], -1)
+    iota("md", T.md[:, 0:576:36], [[0, 16]], -(2 ** 24 - 1))
+    for k in range(len(pairs)):
+        d = worth[k] - worth[k + 1]
+        if d != 1:
+            iota("md", T.md[:, k + 1:576:36], [[0, 16]], -d)
+    iota("nTi", T.nTi[:], [[32, 8], [0, 32]], 1)
+    iota("w256", T.w256[:], [[256, 512]], -65280)
+    iota("w1024", T.w1024[:], [[1024, 272]], 0)
+    iota("xk0", T.xk0[:, 256:264], [[0, 8]], 512)
+    iota("xk1", T.xk1[:, 256:264], [[0, 8]], 512)
     for b in range(4):
-        V("cp", "et", "eye", T.et[:, 512 * b + b:512 * b + 512:4], T.eye[:])
-    V("qz", "eq ep", "et", T.eq[:, 0:512], T.ep[:, 0:512], T.et[:, 0:2048])
-    V("qz", "xq xp", "xt", T.xq[:, 0:256], T.xp[:, 0:256], T.xt[:, 0:1024])
-    V("qz", "uq up", "ut", T.uq[:, 0:128], T.up[:, 0:128], T.ut[:, 0:512])
-    V("ts", "upl", "idw", T.upl[:], T.idw[:, 0:8], 16.0, None, A.mult)
-    V("cp", "uq2", "uq upl", T.uq2[:, 0:128].bitcast(dt.uint32), T.uq[:, 0:128].bitcast(dt.uint32).indirect(T.upl[:, 0:8]))
-    V("cp", "up2", "up upl", T.up2[:, 0:128], T.up[:, 0:128].indirect(T.upl[:, 0:8]))
+        iota("f2z", T.f2[:, 272 * b + 256:272 * b + 272], [[0, 16]], 0)
+    iota("kk", T.kk[:], [[1, 6], [8, 32]], 0)
+    iota("w64", T.w64[:], [[64, 272]], 0)
+    for b in range(4):
+        iota("hbz", T.hb[:, 224 * b + 192:224 * b + 224], [[0, 32]], 0)
+
     V("ts", "pi1", "pi", T.pi[:, 1:2], T.pi[:, 0:1], 15, None, A.bitwise_and)
     V("ts", "pi2", "pi", T.pi[:, 2:3], T.pi[:, 0:1], 31, None, A.bitwise_and)
     V("ts", "pi3", "pi", T.pi[:, 3:4], T.pi[:, 0:1], 4, 1, A.arith_shift_right, A.bitwise_and)
     V("cp", "pf", "pi1 pi2 pi3", T.pf[:, 0:3], T.pi[:, 1:4])
-    V("ts", "pf3", "pf", T.pf[:, 3:4], T.pf[:, 2:3], -1.0, 1.0, A.mult, A.add)
     r16, p32 = T.pf[:, 0:1], T.pf[:, 1:2]
+    V("ts", "sm1", "sm1 pf", T.sm[:, 8:14], T.sm[:, 8:14], r16, None, A.is_equal)
+    V("ts", "sm2", "sm2 pf", T.sm[:, 16:22], T.sm[:, 16:22], r16, None, A.is_equal)
+    V("cp", "upl", "sm0", T.upl[:], T.sm[:, 0:8])
+    V("tt", "sm1", "sm1 sm2", T.sm[:, 8:14], T.sm[:, 8:14], T.sm[:, 16:22], A.add)
+    for b in range(4):
+        V("cp", "et", "eye", T.et[:, 512 * b + b:512 * b + 512:4], T.eye[:])
+    V("qz", "eq ep", "et", T.eq[:, 0:512], T.ep[:, 0:512], T.et[:, 0:2048])
+    V("qz", "uq up", "ut", T.uq[:, 0:128], T.up[:, 0:128], T.ut[:, 0:512])
+    V("cp", "uq2", "uq upl", T.uq2[:, 0:128].bitcast(dt.uint32), T.uq[:, 0:128].bitcast(dt.uint32).indirect(T.upl[:, 0:8]))
+    V("cp", "up2", "up upl", T.up2[:, 0:128], T.up[:, 0:128].indirect(T.upl[:, 0:8]))
+    V("qz", "xq xp", "xt", T.xq[:, 0:256], T.xp[:, 0:256], T.xt[:, 0:1024])
     V("ts", "nmask", "rp pf", T.nmask[:], T.rp[:], r16, -1.0, A.is_equal, A.mult)
     V("ts", "sc0", "rp", T.sc0[:], T.rp[:], 0.0, None, A.not_equal)
-    V("ts", "nw", "nw pf", T.nw[:], T.nw[:], r16, None, A.add)
-    V("ts", "nT", "nT pf", T.nT[:], T.nT[:], p32, None, A.add)
-    V("ts", "kk", "kk", T.kk[:], T.kk[:], 0.125, None, A.mult)
-    V("ts", "scab", "rv", T.scab[:], T.rv[:], 0.0, None, A.not_equal)
-    V("cp", "exl", "idw", T.exl[:], T.idw[:, 0:16])
-    V("ts", "w256", "idw", T.w256[:], T.idw[:], 256.0, -65280.0, A.mult, A.add)
-    V("ts", "w1024", "idw", T.w1024[:], T.idw[:, 0:272], 1024.0, BIG, A.mult, A.min)
-    V("ts", "w64", "idw", T.w64[:], T.idw[:, 0:272], 64.0, None, A.mult)
-    V("ts", "n64", "nw", T.n64[:], T.nw[:], -64.0, None, A.mult)
-    for b in range(2):
-        V("ts", "nm%d" % b, "pf", T.nm[:, b:b + 1], r16, -1024.0, -16384.0 * b, A.mult, A.add)
-        V("ts", "mc%d" % b, "pf", T.mc[:, b:b + 1], r16, 224.0 + 16.0 * b, None, A.add)
     for t, k in enumerate(["v0", "a1", "a2", "a3", "a4", "asc"]):
-        V("ts", "ra", "pf", T.ct[:, 4:5], r16, float(5 - t), None, A.is_equal)
-        V("ts", "rb", "pf", T.ct[:, 5:6], r16, float(8 + t), None, A.is_equal)
-        V("tt", "rb", "ra rb", T.ct[:, 5:6], T.ct[:, 4:5], T.ct[:, 5:6], A.add)
-        V("ts", k, "idw rb", T[k][:], T.idw[:, 0:256], T.ct[:, 5:6], None, A.mult)
-    for kind in range(2):
-        for hh in range(2):
-            e = T.pf[:, 3 - hh:4 - hh]
-            V("ts", "ct%d" % (2 * kind + hh), "pf pf3", T.ct[:, 2 * kind + hh:2 * kind + hh + 1], e, 256.0 * kind - 513.0, 513.0, A.mult, A.add)
-    pairs = [(i, s - i) for s in range(10, 0, -1) for i in range(min(5, s), max(0, s - 5) - 1, -1)]
-    worth = [8 * (i + j) + i for i, j in pairs] + [0]
-    V("memset", "md", "", T.md[:], -1.0 / 128)
-    V("memset", "md", "", T.md[:, 0:576:36], -4.0)
-    for k in range(len(pairs)):
-        d = worth[k] - worth[k + 1]
-        if d != 1:
-            V("memset", "md", "", T.md[:, k + 1:576:36], -d / 128.0)
-    V("memset", "e3", "", T.e3[:, :, 0], 0.0)
-    V("memset", "pq", "", T.pq[:, 512:784], 0.0)
-    V("memset", "pq", "", T.pq[:, 512:513], 256.0)
-    V("memset", "pq", "", T.pq[:, 768:769], 256.0)
-    V("memset", "xk0", "", T.xk0[:, 256:264], 512.0)
-    V("memset", "xk1", "", T.xk1[:, 256:264], 512.0)
-    V("memset", "w2z", "", T.w2[:, :, 0], 0.0)
-    V("memset", "f2z", "", T.f2[:], 0.0)
-    V("memset", "hbz", "", T.hb[:], 0.0)
-    for c in range(16):
-        V("memset", "abz", "", T.abd[:, 200 * c + 192:200 * c + 200], 31.75)
-    V("qz", "vq vp", "vt", T.vq[:, 0:128], T.vp[:, 0:128], T.vt[:, 0:512])
+        S(k, "idw sm1", T[k][:], T.idw[:, 0:256], ACT.Copy, scale=T.sm[:, 8 + t:9 + t])
 
     def lists():
         V("cp", "lw16", "lw lwb", T.lw16[:], T.lw[:])
@@ -222,6 +211,28 @@ def rank_program(g, core, T, topo):
         total["ar%d" % t] = m
         wr["y%d" % t] = ("r", "ar%d" % t, m)
 
+    def late_constants_scalar():
+        S("md", "md", T.md[:], T.md[:], ACT.Copy, scale=1.0 / 128)
+        S("nT", "nTi pf", T.nT[:], T.nTi[:], ACT.Identity, bias=p32, scale=1.0)
+        S("nw", "nw0 pf", T.nw[:], T.sm[:, 32:48], ACT.Identity, bias=r16, scale=1.0)
+        S("n64", "nw", T.n64[:], T.nw[:], ACT.Copy, scale=-64.0)
+        S("sm3", "sm3 pf", T.sm[:, 24:26], T.sm[:, 24:26], ACT.Identity, bias=r16, scale=1.0)
+        S("nm", "sm3", T.nm[:], T.sm[:, 24:26], ACT.Copy, scale=-1024.0)
+        S("kk", "kk", T.kk[:], T.kk[:], ACT.Copy, scale=0.125)
+
+    def late_constants_vector():
+        V("ts", "pf3", "pf", T.pf[:, 3:4], T.pf[:, 2:3], -1.0, 1.0, A.mult, A.add)
+        V("cp", "exl", "exl0", T.exl[:], T.sm[:, 48:64])
+        V("ts", "scab", "rv", T.scab[:], T.rv[:], 0.0, None, A.not_equal)
+        V("ts", "mc", "sm3", T.mc[:], T.sm[:, 24:26], 224.0, None, A.add)
+        for kind in range(2):
+            for hh in range(2):
+                e = T.pf[:, 3 - hh:4 - hh]
+                V("ts", "ct%d" % (2 * kind + hh), "pf pf3", T.ct[:, 2 * kind + hh:2 * kind + hh + 1], e, 256.0 * kind - 513.0, 513.0, A.mult, A.add)
+        V("memset", "w2z", "", T.w2[:, :, 0], 0.0)
+        V("memset", "abz", "", T.abd[:, :, 192:200], 31.75)
+    V("memset", "e3", "", T.e3[:, :, 0], 0.0)
+
     for t in range(R):
         xq, xp = T.xq[:, 0:256], T.xp[:, 0:256]
         for k in ("ps1", "ps2"):
@@ -237,30 +248,32 @@ def rank_program(g, core, T, topo):
         V("tt", "c2", "c1 lw lwb", T.cf[:, 32:48], T.cf[:, 16:32], T.lw[:, 0:16], A.add)
         V("cp", "wc16", "c2", T.wc16[:], T.cf[:, 32:48])
         for c in range(16):
+            if t == 0 and c == 4:
+                late_constants_scalar()
             S("jk%d acc%d" % (c, c), "ssb sc", T.jk[:, 256 * c:256 * c + 256], T.ssb[:], ACT.Sign, bias=T.sc[:, 16 * c + 15:16 * c + 16], scale=1.0, accum_out=T.acc[:, c:c + 1])
         cur = "v0"
         for k, add in enumerate(["a1", "a2", "a3", "a4", "asc"]):
             nxt = "va" if k % 2 == 0 else "vb"
             V("tt", nxt, cur + " wc16 " + add, T[nxt][:], T[cur][:, 0:256].indirect(T.wc16[:, 0:16]), T[add][:], A.add)
             cur = nxt
-        V("cp", "pq0", cur + " lw16 pq", T.pq[:, 0:256], T[cur][:, 0:256].indirect(T.lw16[:, 0:16]))
-        V("cp", "pq1", cur + " lw16 pq", T.pq[:, 256:512], T[cur][:, 0:256].indirect(T.lw16[:, 16:32]))
-        V("tr", "t3", "pq0 pq1", T.t3[:], T.pq[:, 0:512])
+        V("cp", "pq0", cur + " lw16 pq", T.pq[:, 0:512], T[cur][:, 0:256].indirect(T.lw16[:, 0:32]))
+        V("tr", "t3", "pq0", T.t3[:], T.pq[:, 0:512])
         k = 1
         for s in range(10, 0, -1):
             hi, lo = min(5, s), max(0, s - 5)
             n = hi - lo + 1
             V("tt", "e3_%d" % s, "t3 e3", T.e3[:, :, k:k + n], T.t3[:, 0:16, 13 - hi:14 - lo], T.t3[:, 16:32, s - hi:s - lo + 1], A.is_equal)
             k += n
-        V("tt", "ne", "t3", T.ne[:], T.t3[:, 0:16, 0], T.t3[:, 16:32, 0], A.not_equal)
-        V("cp", "e2", "e3 " + " ".join("e3_%d" % s for s in range(1, 11)), T.e2[:], T.e3[:])
-        V("scan", "so", "e2 md", T.so[:], T.e2[:], T.md[:], 0.0, A.max, A.add)
-        V("tt", "hit", "so ne", T.hit[:, 0:16], T.so[:, 35:576:36], T.ne[:], A.mult)
-        V("ts", "hy", "hit", T.hit[:, 16:32], T.hit[:, 0:16], 0.0, BIG, A.is_le, A.mult)
-        V("tt", "yv", "hy hit", T.yv[:], T.hit[:, 16:32], T.hit[:, 0:16], A.subtract)
+        V("tt", "ne", "t3", T.ne[:, 0:16], T.t3[:, 0:16, 0], T.t3[:, 16:32, 0], A.is_equal)
+        V("ts", "e2", "e3 " + " ".join("e3_%d" % s for s in range(1, 11)), T.e2[:], T.e3[:], BIG, 1.0 - BIG, A.mult, A.add)
+        V("ts", "neb", "ne", T.ne[:, 16:32], T.ne[:, 0:16], BIG, None, A.mult)
+        V("scan", "so", "e2 md", T.so[:], T.e2[:], T.md[:], -BIG, A.max, A.add)
+        if t == 0:
+            late_constants_vector()
+        accs = " ".join("acc%d" % c for c in range(16))
+        V("tt", "yv", "neb so", T.yv[:], T.ne[:, 16:32], T.so[:, 35:576:36], A.subtract)
         V("tt", "ex", "yv exl nT", T.ex[:], T.yv[:, 0:16].indirect(T.exl[:, 0:16]), T.nT[:], A.add)
         V("tr", "ur", "ex", T.ur[:], T.ex[:])
-        accs = " ".join("acc%d" % c for c in range(16))
         V("ts", "a16", accs, T.a16[:], T.acc[:], 255.0, None, A.add)
         V("ts", "nb0", accs, T.nB[:, 16:32], T.acc[:], -256.0, None, A.mult)
         V("tt", "kap", "a16 w256 ur", T.kap[:], T.w256[:, 0:512].indirect(T.a16[:, 0:16]), T.ur[:], A.add)
@@ -274,12 +287,14 @@ def rank_program(g, core, T, topo):
         V("cp", "r16b", " ".join("rk%d" % c for c in range(NS, 16)), T.r16[:, NS:16], T.acc2[:, NS:16])
         V("ts", "r16a", " ".join("rk%d" % c for c in range(NS)), T.r16[:, 0:NS], T.acc2[:, 0:NS], -0.5, 128.0, A.mult, A.add)
         V("tt", "qq", "r16a r16b w1024 ur", T.qq[:], T.w1024[:, 0:272].indirect(T.r16[:, 0:16]), T.ur[:], A.add)
-        S("xk1a", "qq nm1", T.xk1[:, 0:256], T.qq[:], ACT.Identity, bias=T.nm[:, 1:2], scale=1.0)
-        V("ts", "xk0a", "qq nm0", T.xk0[:, 0:256], T.qq[:], T.nm[:, 0:1], None, A.add)
+        S("xk1a", "qq nm", T.xk1[:, 0:256], T.qq[:], ACT.Identity, bias=T.nm[:, 1:2], scale=1.0)
+        V("ts", "xk0a", "qq nm", T.xk0[:, 0:256], T.qq[:], T.nm[:, 0:1], None, A.add)
         V("red", "kv0", "xk0 xk0a", T.kv[:, 0:1], T.xk0[:, 0:264], XAX, A.min, apply_absolute_value=True)
         V("red", "kv1", "xk1 xk1a", T.kv[:, 1:2], T.xk1[:, 0:264], XAX, A.min, apply_absolute_value=True)
         for b in range(4):
             S("f2_%d" % b, "pd%d f2z" % b, T.f2[:, 272 * b:272 * b + 256], T["pd%d" % b][:, 0:256], ACT.Copy, scale=0.5)
+        for b in range(4):
+            S("fw%d" % b, "pd%d" % b, T.fw[:, 256 * b:256 * b + 256], T["pd%d" % b][:, 0:256], ACT.Copy)
         V("ts", "kq", "kv0 kv1", T.kq[:], T.kv[:], 128.0, None, A.mult)
         V("ts", "kn", "kq", T.kn[:], T.kq[:], 7, None, A.arith_shift_right)
         V("ts", "ij0", "kq", T.ij[:, 0:2], T.kq[:], 7, None, A.bitwise_and)
@@ -289,7 +304,7 @@ def rank_program(g, core, T, topo):
                 o = 4 * kind + hh
                 c = 2 * kind + hh
                 V("ts", "off%d" % o, "kn pf pf3 ct%d" % c, T.off[:, o:o + 3:2], T.kn[:], T.pf[:, 3 - hh:4 - hh], T.ct[:, c:c + 1], A.mult, A.add)
-        V("cp", "g2", "pq pq0 pq1 off0 off1 off4 off5", T.g2[:], T.pq[:, 0:784].indirect(T.off[:, 0:8]))
+        V("cp", "g2", "pq pq0 off0 off1 off4 off5", T.g2[:], T.pq[:, 0:784].indirect(T.off[:, 0:8]))
         V("tt", "ij1", "sij ij0", T.ij[:, 2:4], T.ij[:, 4:6], T.ij[:, 0:2], A.subtract)
         V("tr", "t2", "g2", T.t2[:], T.g2[:])
         V("cp", "ijf", "ij0 ij1", T.ijf[:], T.ij[:, 0:4])
@@ -303,29 +318,27 @@ def rank_program(g, core, T, topo):
             for b in range(2):
                 o = 12 * kind
                 V("cp", "ab16_%d%d" % (kind, b), "ab", T.ab16[:, o + b:o + 12:2], T.ab[:, o + 6 * b:o + 6 * b + 6])
+        V("tt", "br", "w2", T.br[:], T.w2[:, 2:4, 16], T.w2[:, 0:2, 16], A.is_gt)
+        V("tt", "dba", "ab", T.dba[:], T.ab[:, 12:24], T.ab[:, 0:12], A.subtract)
+        for b in range(2):
+            V("ts", "bt_%d" % b, "dba br", T.bt[:, 6 * b:6 * b + 6], T.dba[:, 6 * b:6 * b + 6], T.br[:, b:b + 1], None, A.mult)
         for b in range(4):
             S("at%d" % b, "f2z f2_%d ab16_00 ab16_01" % b, T.at[:, 192 * b:192 * b + 192], T.f2[:, 272 * b:272 * b + 272].indirect(T.ab16[:, 0:12]), ACT.Copy)
             V("tt", "zt%d" % b, "f2z f2_%d ab16_10 ab16_11 at%d" % (b, b), T.zt[:, b:768:4], T.f2[:, 272 * b:272 * b + 272].indirect(T.ab16[:, 12:24]), T.at[:, 192 * b:192 * b + 192], A.add)
         V("qz", "zq zp", "zt0 zt1 zt2 zt3", T.zq[:, 0:192], T.zp[:, 0:192], T.zt[:, 0:768])
         send(t)
-        V("tt", "br", "w2", T.br[:], T.w2[:, 2:4, 16], T.w2[:, 0:2, 16], A.is_gt)
-        V("tt", "dba", "ab", T.dba[:], T.ab[:, 12:24], T.ab[:, 0:12], A.subtract)
-        for b in range(2):
-            V("ts", "bt_%d" % b, "dba br", T.bt[:, 6 * b:6 * b + 6], T.dba[:, 6 * b:6 * b + 6], T.br[:, b:b + 1], None, A.mult)
         V("tt", "dba", "bt_0 bt_1 ab", T.dba[:], T.bt[:], T.ab[:, 0:12], A.add)
         for b in range(2):
             V("cp", "bt16_%d" % b, "dba", T.bt16[:, b:12:2], T.dba[:, 6 * b:6 * b + 6])
         V("tt", "ke", "bt16_0 bt16_1 w64 kk", T.ke[:], T.w64[:, 0:272].indirect(T.bt16[:, 0:12]), T.kk[:], A.add)
-        for b in range(4):
-            S("fw%d" % b, "pd%d" % b, T.fw[:, 256 * b:256 * b + 256], T["pd%d" % b][:, 0:256], ACT.Copy)
         for c in range(16):
-            S("abd%d" % c, "ke n64 abz", T.abd[:, 200 * c:200 * c + 192], T.ke[:], ACT.Abs, bias=T.n64[:, c:c + 1], scale=1.0)
+            S("abd%d" % c, "ke n64 abz", T.abd[:, c, 0:192], T.ke[:], ACT.Abs, bias=T.n64[:, c:c + 1], scale=1.0)
         V("ts", "li0", "kn", T.li[:, 0:2], T.kn[:], 15, None, A.bitwise_and)
         V("ts", "li1", "kn", T.li[:, 2:4], T.kn[:], 4, None, A.arith_shift_right)
         V("ts", "li2", "kn", T.li[:, 4:6], T.kn[:], 9, None, A.arith_shift_right)
         V("ts", "li3", "li0", T.li[:, 6:8], T.li[:, 0:2], 16.0, 256.0, A.mult, A.add)
         V("ts", "li4", "br", T.li[:, 8:10], T.br[:], -256.0, None, A.mult)
-        V("tt", "li5", "li2 mc0 mc1", T.li[:, 10:12], T.li[:, 4:6], T.mc[:], A.mult)
+        V("tt", "li5", "li2 mc", T.li[:, 10:12], T.li[:, 4:6], T.mc[:], A.mult)
         V("tt", "li6", "li3 li1", T.li[:, 12:14], T.li[:, 6:8], T.li[:, 2:4], A.add)
         V("tt", "li7", "li4 li5", T.li[:, 14:16], T.li[:, 8:10], T.li[:, 10:12], A.add)
         V("tt", "li8", "li6 li7", T.li[:, 16:18], T.li[:, 12:14], T.li[:, 14:16], A.add)
@@ -334,26 +347,31 @@ def rank_program(g, core, T, topo):
         V("cp", "lt0 lt1", "mt ln16", T.lt[:, 0:560].indirect(T.ln16[:, 0:2]), T.mt[:])
         dma("y", "dl0", ["lt0"], ["lw"], T.lw[:, 0:16], T.lt[0:128:16, 0:256])
         dma("y", "dl1", ["lt1"], ["lwb"], T.lw[:, 16:32], T.lt[0:128:16, 256:512])
+        if t == 0:
+            V("qz", "vq vp", "vt", T.vq[:, 0:128], T.vp[:, 0:128], T.vt[:, 0:512])
         for c in range(16):
-            V("red", "ev%d" % c, "abz abd%d" % c, T.ev[:, c:c + 1], T.abd[:, 200 * c:200 * c + 193], XAX, A.min)
+            V("red", "ev%d" % c, "abz abd%d" % c, T.ev[:, c:c + 1], T.abd[:, c, 0:193], XAX, A.min)
         V("ts", "ei", " ".join("ev%d" % c for c in range(16)), T.ei[:, 0:16], T.ev[:], 256.0, None, A.mult)
         V("ts", "ek", "ei", T.ei[:, 16:32], T.ei[:, 0:16], 255, None, A.bitwise_and)
         V("ts", "em", "ei", T.ei[:, 32:48], T.ei[:, 0:16], 8, None, A.arith_shift_right)
         V("tt", "ex2", "ek em", T.ei[:, 48:64], T.ei[:, 16:32], T.ei[:, 32:48], A.add)
         V("cp", "e16", "ex2", T.e16[:], T.ei[:, 48:64])
+        if t == R - 1:
+            V("cp", "lw16", "lw lwb", T.lw16[:], T.lw[:])
         ph = ["ph0", "ph1", "ps1", "ps2"]
         for b in range(4):
             mm(ph[b], T.wq[:, 128 * b:128 * b + 128], "wq wp", T.wp[:, 128 * b:128 * b + 128], T["yq%d" % t][:, 0:192], "y%d" % t, T["yp%d" % t][:, 0:192], 192)
             S("hb%d" % b, ph[b] + " hbz", T.hb[:, 224 * b:224 * b + 192], T[ph[b]][:, 0:192], ACT.Copy, scale=0.03125)
             V("tt", "xs%d" % b, "hbz hb%d e16 fw%d" % (b, b), T.xs[:, b:1024:4], T.hb[:, 224 * b:224 * b + 224].indirect(T.e16[:, 0:16]), T.fw[:, 256 * b:256 * b + 256], A.add)
         V("qz", "xq xp", "xs0 xs1 xs2 xs3", T.xq[:, 0:256], T.xp[:, 0:256], T.xs[:, 0:1024])
-        lists()
+        if t < R - 1:
+            lists()
+    S("olr", "idw lw16", T.olr[:], T.idw[:, 0:256].indirect(T.lw16[:, 0:32]), ACT.Copy)
+    dma("y", "ool", ["olr"], [], T.ol[:], T.olr[0:128:16, :])
+    mm("ps1", T.vq[:, 0:128], "vq vp", T.vp[:, 0:128], T.xq[:, 0:256], "xq xp", T.xp[:, 0:256], 256)
     dma("y", "ooc", ["xq"], [], T.oc[:, 0:1024], T.xq[:, 0:256].bitcast(dt.uint8))
     for k in range(4):
-        dma("y" if k % 2 else "s", "os%d" % k, ["xp"], [], T.osc[4 * k:4 * k + 4, 0:256], T.xp[32 * k:32 * k + 4, 0:256])
-    mm("ps1", T.vq[:, 0:128], "vq vp", T.vp[:, 0:128], T.xq[:, 0:256], "xq xp", T.xp[:, 0:256], 256)
+        dma("y", "os%d" % k, ["xp"], [], T.osc[4 * k:4 * k + 4, 0:256], T.xp[32 * k:32 * k + 4, 0:256])
     S("ysb", "ps1", T.ysb[:], T.ps1[:, 0:256], ACT.Copy)
     dma("s", "oy", ["ysb"], [], T.y[:], T.ysb[:])
-    V("cp", "olr", "idw lw16", T.olr[:], T.idw[:, 0:256].indirect(T.lw16[:, 0:32]))
-    dma("y", "ool", ["olr"], [], T.ol[:], T.olr[0:128:16, :])
     need("g", [(s, n) for s, n in total.items()])

@@ -4,7 +4,7 @@ from concourse.mybir import dt, AluOpType, ActivationFunctionType, AxisListType
 N = 8
 R = 3
 C = 256
-NS = 10
+NS = 11
 BIG = 131072.0
 F32, BF, I32, U16, U8, X4 = "float32", "bfloat16", "int32", "uint16", "uint8", "float8_e4m3fn_x4"
 
@@ -22,30 +22,31 @@ SCRATCH = {
     "zt": _sb(768, BF), "zq": _sb(192, X4), "zp": _sb(192, U8),
     "pi": _sb(4, I32), "pf": _sb(4, F32), "sm": _sb(64, F32), "idw": _sb(512, F32), "rp": _sb(256, F32), "nmask": _sb(256, F32),
     "sc0": _sb(256, F32), "nw": _sb(16, F32), "nT": _sb(256, F32), "nTi": _sb(256, F32), "kk": _sb(192, F32), "rv": _sb(24, F32),
-    "scab": _sb(24, F32), "exl": _sb(16, U16), "upl": _sb(8, U16), "w256": _sb(512, F32), "w1024": _sb(272, F32),
-    "w64": _sb(272, F32), "n64": _sb(16, F32), "nm": _sb(2, F32), "mc": _sb(2, F32), "md": _sb(576, F32),
+    "scab": _sb(24, F32), "exl": _sb(16, U16), "upl": _sb(8, U16), "w256": _sb(512, F32), "w2048": _sb(272, F32),
+    "w512": _sb(272, F32), "n512": _sb(16, F32), "nm": _sb(2, F32), "md": _sb(576, F32), "gm": _sb(64, F32),
+    "cl": _sb(160, F32), "cl2": _sb(160, F32), "cl16": _sb(10, U16),
     "v0": _sb(256, F32), "a1": _sb(256, F32), "a2": _sb(256, F32), "a3": _sb(256, F32), "a4": _sb(256, F32),
-    "asc": _sb(256, F32), "ct": _sb(4, F32),
+    "asc": _sb(256, F32),
     "ms": _sb(256, F32), "sc": _sb(256, F32), "ssb": _sb(256, F32), "cf": _sb(48, F32),
-    "wc16": _sb(16, U16), "va": _sb(256, F32), "vb": _sb(256, F32), "pq": _sb(784, F32),
+    "wc16": _sb(16, U16), "va": _sb(256, F32), "vb": _sb(256, F32), "pq": _sb(1280, F32),
     "t3": ("sbuf", [128, 32, 16], F32), "e3": ("sbuf", [128, 16, 36], BF), "e2": _sb(576, BF), "so": _sb(576, F32),
     "ne": _sb(32, F32), "yv": _sb(16, F32), "ex": _sb(256, F32),
     "ur": _sb(256, F32), "jk": _sb(4096, BF), "acc": _sb(16, F32), "acc2": _sb(16, F32),
     "a16": _sb(16, U16), "nB": _sb(32, F32), "kap": _sb(256, F32), "r16": _sb(16, U16),
-    "qq": _sb(256, F32), "xk0": _sb(264, F32), "xk1": _sb(264, F32), "kv": _sb(2, F32), "kq": _sb(2, I32),
-    "kn": _sb(2, I32), "off": _sb(8, U16), "g2": _sb(128, F32), "t2": ("sbuf", [128, 8, 16], F32),
-    "w2": ("sbuf", [128, 4, 20], F32), "ij": _sb(8, I32), "ijf": _sb(4, F32),
-    "ff": ("sbuf", [128, 4, 6], F32), "dd": ("sbuf", [128, 4, 6], F32), "d2": _sb(24, F32), "ab": _sb(24, F32),
-    "ab16": _sb(24, U16), "br": _sb(2, F32), "dba": _sb(12, F32), "bt": _sb(12, F32), "bt16": _sb(12, U16),
+    "qq": _sb(256, F32), "xk0": _sb(264, F32), "xk1": _sb(264, F32), "kv": _sb(2, F32), "kw": _sb(32, I32),
+    "kn": _sb(16, I32), "off": _sb(4, U16), "g2": _sb(128, F32), "t2": ("sbuf", [128, 8, 16], F32),
+    "w2": ("sbuf", [128, 4, 20], F32), "ij": _sb(24, I32),
+    "ff": _sb(24, F32), "dd": _sb(24, F32), "d2": _sb(24, F32), "ab": _sb(24, F32),
+    "ab16": _sb(32, U16), "br": _sb(2, F32), "dba": _sb(16, F32), "bt": _sb(16, F32), "bt16": _sb(16, U16),
     "ke": _sb(192, F32), "abd": ("sbuf", [128, 16, 200], F32), "ev": _sb(16, F32), "ei": _sb(64, I32), "e16": _sb(16, U16),
-    "li": _sb(20, I32), "ln16": _sb(2, U16), "mt": _sb(32, I32), "lt": _sb(560, I32), "lw": _sb(32, I32),
+    "li": _sb(12, I32), "ln16": _sb(2, U16), "mt": _sb(32, I32), "lt": _sb(560, I32), "lw": _sb(32, I32),
     "lw16": _sb(32, U16), "dl": _sb(16, F32), "olr": _sb(512, F32), "ysb": _sb(256, F32),
     "at": _sb(768, BF), "f2": _sb(1088, BF), "fw": _sb(1024, BF), "hb": _sb(896, F32),
 }
+PS = ["ps1", "ps2", "pd0", "pd1", "pd2", "pd3", "ph0", "ph1"]
 for _t in range(R):
     SCRATCH["yq%d" % _t] = _sb(192, X4)
     SCRATCH["yp%d" % _t] = _sb(192, U8)
-PS = ["ps1", "ps2", "pd0", "pd1", "pd2", "pd3", "ph0", "ph1"]
 for _n in PS:
     SCRATCH[_n] = ("psum", [128, 512], F32)
 
@@ -136,13 +137,8 @@ def rank_program(g, core, T, topo):
     op("g", ["one"], ["eye"], "asel", T.eye[:], T.one[:], [[-1, 128]], A.is_equal, 0.0, 0, 1)
     iota("idw", T.idw[:], [[1, 512]], 0)
     iota("rp", T.rp[:], [[0, 16], [1, 16]], 0)
-    iota("sm3", T.sm[:, 24:26], [[16, 2]], 0)
-    iota("rv", T.rv[:], [[0, 4], [1, 6]], 0)
     iota("nw0", T.sm[:, 32:48], [[16, 16]], 0)
     iota("exl0", T.sm[:, 48:64], [[1, 16]], 0)
-    iota("pq", T.pq[:, 512:784], [[0, 272]], 0)
-    iota("pq", T.pq[:, 512:513], [[0, 1]], 256)
-    iota("pq", T.pq[:, 768:769], [[0, 1]], 256)
     pairs = [(i, s - i) for s in range(10, 0, -1) for i in range(min(5, s), max(0, s - 5) - 1, -1)]
     worth = [8 * (i + j) + i for i, j in pairs] + [0]
     iota("md", T.md[:], [[0, 576]], -1)
@@ -153,13 +149,24 @@ def rank_program(g, core, T, topo):
             iota("md", T.md[:, k + 1:576:36], [[0, 16]], -d)
     iota("nTi", T.nTi[:], [[32, 8], [0, 32]], 1)
     iota("w256", T.w256[:], [[256, 512]], -65280)
-    iota("w1024", T.w1024[:], [[1024, 272]], 0)
-    iota("xk0", T.xk0[:, 256:264], [[0, 8]], 512)
-    iota("xk1", T.xk1[:, 256:264], [[0, 8]], 512)
+    iota("w2048", T.w2048[:], [[2048, 272]], 0)
+    iota("sm3", T.sm[:, 24:26], [[16, 2]], 0)
+    iota("xk0", T.xk0[:, 256:264], [[0, 8]], 527)
+    iota("xk1", T.xk1[:, 256:264], [[0, 8]], 783)
+    iota("rv", T.rv[:], [[0, 4], [1, 6]], 0)
+    iota("gm", T.gm[:], [[0, 2], [1, 2], [0, 16]], 0)
+    iota("cl", T.cl[:], [[0, 160]], 0)
+    iota("cl", T.cl[:, 0:16], [[0, 4], [1, 2], [0, 2]], 0)
+    iota("cl", T.cl[:, 32:56], [[0, 2], [1, 2], [0, 6]], 0)
+    iota("cl", T.cl[:, 64:88], [[12, 2], [1, 6], [6, 2]], 0)
+    iota("cl", T.cl[:, 96:108], [[1, 2], [0, 6]], 0)
+    iota("cl", T.cl[:, 128:140], [[1, 6], [6, 2]], 0)
+    iota("pqz", T.pq[:, 512:1280], [[0, 768]], 256)
     for b in range(4):
         iota("f2z", T.f2[:, 272 * b + 256:272 * b + 272], [[0, 16]], 0)
+    iota("dbz", T.dba[:, 12:16], [[0, 4]], 0)
     iota("kk", T.kk[:], [[1, 6], [8, 32]], 0)
-    iota("w64", T.w64[:], [[64, 272]], 0)
+    iota("w512", T.w512[:], [[512, 272]], 0)
     for b in range(4):
         iota("hbz", T.hb[:, 224 * b + 192:224 * b + 224], [[0, 32]], 0)
 
@@ -173,8 +180,7 @@ def rank_program(g, core, T, topo):
     V("cp", "upl", "sm0", T.upl[:], T.sm[:, 0:8])
     V("tt", "sm1", "sm1 sm2", T.sm[:, 8:14], T.sm[:, 8:14], T.sm[:, 16:22], A.add)
     for b in range(4):
-        V("cp", "et", "eye", T.et[:, 512 * b + b:512 * b + 512:4], T.eye[:])
-    V("qz", "eq ep", "et", T.eq[:, 0:512], T.ep[:, 0:512], T.et[:, 0:2048])
+        S("et", "eye", T.et[:, 512 * b + b:512 * b + 512:4], T.eye[:], ACT.Copy)
     V("qz", "uq up", "ut", T.uq[:, 0:128], T.up[:, 0:128], T.ut[:, 0:512])
     V("cp", "uq2", "uq upl", T.uq2[:, 0:128].bitcast(dt.uint32), T.uq[:, 0:128].bitcast(dt.uint32).indirect(T.upl[:, 0:8]))
     V("cp", "up2", "up upl", T.up2[:, 0:128], T.up[:, 0:128].indirect(T.upl[:, 0:8]))
@@ -211,32 +217,34 @@ def rank_program(g, core, T, topo):
         total["ar%d" % t] = m
         wr["y%d" % t] = ("r", "ar%d" % t, m)
 
-    def late_constants_scalar():
+    def late_constants():
         S("md", "md", T.md[:], T.md[:], ACT.Copy, scale=1.0 / 128)
         S("nT", "nTi pf", T.nT[:], T.nTi[:], ACT.Identity, bias=p32, scale=1.0)
         S("nw", "nw0 pf", T.nw[:], T.sm[:, 32:48], ACT.Identity, bias=r16, scale=1.0)
-        S("n64", "nw", T.n64[:], T.nw[:], ACT.Copy, scale=-64.0)
+        S("n512", "nw", T.n512[:], T.nw[:], ACT.Copy, scale=-512.0)
         S("sm3", "sm3 pf", T.sm[:, 24:26], T.sm[:, 24:26], ACT.Identity, bias=r16, scale=1.0)
-        S("nm", "sm3", T.nm[:], T.sm[:, 24:26], ACT.Copy, scale=-1024.0)
-        S("kk", "kk", T.kk[:], T.kk[:], ACT.Copy, scale=0.125)
-
-    def late_constants_vector():
-        V("ts", "pf3", "pf", T.pf[:, 3:4], T.pf[:, 2:3], -1.0, 1.0, A.mult, A.add)
+        S("nm", "sm3", T.nm[:], T.sm[:, 24:26], ACT.Copy, scale=-2048.0)
+        S("sm4", "pf", T.sm[:, 28:29], r16, ACT.Copy, scale=16.0)
+        for k in ("xk0", "xk1"):
+            S(k, k + " sm4", T[k][:, 256:264], T[k][:, 256:264], ACT.Identity, bias=T.sm[:, 28:29], scale=1.0)
         V("cp", "exl", "exl0", T.exl[:], T.sm[:, 48:64])
+
+    def later_constants():
         V("ts", "scab", "rv", T.scab[:], T.rv[:], 0.0, None, A.not_equal)
-        V("ts", "mc", "sm3", T.mc[:], T.sm[:, 24:26], 224.0, None, A.add)
-        for kind in range(2):
-            for hh in range(2):
-                e = T.pf[:, 3 - hh:4 - hh]
-                V("ts", "ct%d" % (2 * kind + hh), "pf pf3", T.ct[:, 2 * kind + hh:2 * kind + hh + 1], e, 256.0 * kind - 513.0, 513.0, A.mult, A.add)
+        V("ts", "gm", "gm pf", T.gm[:], T.gm[:], T.pf[:, 2:3], None, A.is_equal)
+        V("tt", "cl2", "cl nmask", T.cl2[:], T.cl[:], T.nmask[:, 0:160], A.mult)
+        V("scan", "cl", "cl2 sc0", T.cl[:], T.sc0[:, 0:160], T.cl2[:], 0.0, A.mult, A.add)
+        V("ts", "cl16", "cl", T.cl16[:], T.cl[:, 15:160:16], -1.0, None, A.mult)
         V("memset", "w2z", "", T.w2[:, :, 0], 0.0)
-        V("memset", "abz", "", T.abd[:, :, 192:200], 31.75)
+        V("memset", "abz", "", T.abd[:, :, 192:200], 254.0)
     V("memset", "e3", "", T.e3[:, :, 0], 0.0)
 
     for t in range(R):
         xq, xp = T.xq[:, 0:256], T.xp[:, 0:256]
         for k in ("ps1", "ps2"):
             mm(k, T.uq2[:, 0:128], "uq2 up2", T.up2[:, 0:128], xq, "xq xp", xp, 256)
+        if t == 0:
+            V("qz", "eq ep", "et", T.eq[:, 0:512], T.ep[:, 0:512], T.et[:, 0:2048])
         for b in range(4):
             mm("pd%d" % b, T.eq[:, 128 * b:128 * b + 128], "eq ep", T.ep[:, 128 * b:128 * b + 128], xq, "xq xp", xp, 256)
         V("tt", "ms", "ps1 nmask", T.ms[:], T.ps1[:, 0:256], T.nmask[:], A.mult)
@@ -247,17 +255,22 @@ def rank_program(g, core, T, topo):
         V("tt", "c1", "cf dl", T.cf[:, 16:32], T.cf[:, 0:16], T.dl[:], A.mult)
         V("tt", "c2", "c1 lw lwb", T.cf[:, 32:48], T.cf[:, 16:32], T.lw[:, 0:16], A.add)
         V("cp", "wc16", "c2", T.wc16[:], T.cf[:, 32:48])
-        for c in range(16):
-            if t == 0 and c == 4:
-                late_constants_scalar()
-            S("jk%d acc%d" % (c, c), "ssb sc", T.jk[:, 256 * c:256 * c + 256], T.ssb[:], ACT.Sign, bias=T.sc[:, 16 * c + 15:16 * c + 16], scale=1.0, accum_out=T.acc[:, c:c + 1])
+
+        def order(lo, hi):
+            for c in range(lo, hi):
+                S("jk%d acc%d" % (c, c), "ssb sc", T.jk[:, 256 * c:256 * c + 256], T.ssb[:], ACT.Sign, bias=T.sc[:, 16 * c + 15:16 * c + 16], scale=1.0, accum_out=T.acc[:, c:c + 1])
+        order(0, 11)
         cur = "v0"
         for k, add in enumerate(["a1", "a2", "a3", "a4", "asc"]):
             nxt = "va" if k % 2 == 0 else "vb"
             V("tt", nxt, cur + " wc16 " + add, T[nxt][:], T[cur][:, 0:256].indirect(T.wc16[:, 0:16]), T[add][:], A.add)
             cur = nxt
-        V("cp", "pq0", cur + " lw16 pq", T.pq[:, 0:512], T[cur][:, 0:256].indirect(T.lw16[:, 0:32]))
-        V("tr", "t3", "pq0", T.t3[:], T.pq[:, 0:512])
+        V("cp", "pq0", cur + " lw16", T.pq[:, 0:256], T[cur][:, 0:256].indirect(T.lw16[:, 0:16]))
+        S("pq1", cur + " lw16", T.pq[:, 256:512], T[cur][:, 0:256].indirect(T.lw16[:, 16:32]), ACT.Copy)
+        order(11, 16)
+        V("tr", "t3", "pq0 pq1", T.t3[:], T.pq[:, 0:512])
+        if t == 0:
+            late_constants()
         k = 1
         for s in range(10, 0, -1):
             hi, lo = min(5, s), max(0, s - 5)
@@ -268,8 +281,6 @@ def rank_program(g, core, T, topo):
         V("ts", "e2", "e3 " + " ".join("e3_%d" % s for s in range(1, 11)), T.e2[:], T.e3[:], BIG, 1.0 - BIG, A.mult, A.add)
         V("ts", "neb", "ne", T.ne[:, 16:32], T.ne[:, 0:16], BIG, None, A.mult)
         V("scan", "so", "e2 md", T.so[:], T.e2[:], T.md[:], -BIG, A.max, A.add)
-        if t == 0:
-            late_constants_vector()
         accs = " ".join("acc%d" % c for c in range(16))
         V("tt", "yv", "neb so", T.yv[:], T.ne[:, 16:32], T.so[:, 35:576:36], A.subtract)
         V("tt", "ex", "yv exl nT", T.ex[:], T.yv[:, 0:16].indirect(T.exl[:, 0:16]), T.nT[:], A.add)
@@ -285,8 +296,10 @@ def rank_program(g, core, T, topo):
         for c in range(NS, 16):
             V("red", "rk%d" % c, "jk%d" % c, T.acc2[:, c:c + 1], T.jk[:, 256 * c:256 * c + 256], XAX, A.add)
         V("cp", "r16b", " ".join("rk%d" % c for c in range(NS, 16)), T.r16[:, NS:16], T.acc2[:, NS:16])
+        if t == 0:
+            later_constants()
         V("ts", "r16a", " ".join("rk%d" % c for c in range(NS)), T.r16[:, 0:NS], T.acc2[:, 0:NS], -0.5, 128.0, A.mult, A.add)
-        V("tt", "qq", "r16a r16b w1024 ur", T.qq[:], T.w1024[:, 0:272].indirect(T.r16[:, 0:16]), T.ur[:], A.add)
+        V("tt", "qq", "r16a r16b w2048 ur", T.qq[:], T.w2048[:, 0:272].indirect(T.r16[:, 0:16]), T.ur[:], A.add)
         S("xk1a", "qq nm", T.xk1[:, 0:256], T.qq[:], ACT.Identity, bias=T.nm[:, 1:2], scale=1.0)
         V("ts", "xk0a", "qq nm", T.xk0[:, 0:256], T.qq[:], T.nm[:, 0:1], None, A.add)
         V("red", "kv0", "xk0 xk0a", T.kv[:, 0:1], T.xk0[:, 0:264], XAX, A.min, apply_absolute_value=True)
@@ -295,55 +308,42 @@ def rank_program(g, core, T, topo):
             S("f2_%d" % b, "pd%d f2z" % b, T.f2[:, 272 * b:272 * b + 256], T["pd%d" % b][:, 0:256], ACT.Copy, scale=0.5)
         for b in range(4):
             S("fw%d" % b, "pd%d" % b, T.fw[:, 256 * b:256 * b + 256], T["pd%d" % b][:, 0:256], ACT.Copy)
-        V("ts", "kq", "kv0 kv1", T.kq[:], T.kv[:], 128.0, None, A.mult)
-        V("ts", "kn", "kq", T.kn[:], T.kq[:], 7, None, A.arith_shift_right)
-        V("ts", "ij0", "kq", T.ij[:, 0:2], T.kq[:], 7, None, A.bitwise_and)
-        V("ts", "sij", "kq", T.ij[:, 4:6], T.kq[:], 3, 15, A.arith_shift_right, A.bitwise_and)
+        V("ts", "kn", "kv0 kv1 cl16", T.kn[:], T.kv[:, 0:2].indirect(T.cl16[:, 0:1]), -0.34, None, A.add)
+        V("ts", "kw", "kv0 kv1 cl16", T.kw[:], T.kv[:, 0:2].indirect(T.cl16[:, 2:4]), 128.0, None, A.mult)
+        V("cp", "off", "kn", T.off[:], T.kn[:, 0:4])
+        V("ts", "ij", "kw", T.ij[:], T.kw[:, 0:24], 7, None, A.bitwise_and)
         for kind in range(2):
-            for hh in range(2):
-                o = 4 * kind + hh
-                c = 2 * kind + hh
-                V("ts", "off%d" % o, "kn pf pf3 ct%d" % c, T.off[:, o:o + 3:2], T.kn[:], T.pf[:, 3 - hh:4 - hh], T.ct[:, c:c + 1], A.mult, A.add)
-        V("cp", "g2", "pq pq0 off0 off1 off4 off5", T.g2[:], T.pq[:, 0:784].indirect(T.off[:, 0:8]))
-        V("tt", "ij1", "sij ij0", T.ij[:, 2:4], T.ij[:, 4:6], T.ij[:, 0:2], A.subtract)
-        V("tr", "t2", "g2", T.t2[:], T.g2[:])
-        V("cp", "ijf", "ij0 ij1", T.ijf[:], T.ij[:, 0:4])
+            V("tt", "g2_%d" % kind, "pqz pq0 pq1 off gm", T.g2[:, 64 * kind:64 * kind + 64], T.pq[:, 256 * kind:256 * kind + 1024].indirect(T.off[:, 0:4]), T.gm[:], A.mult)
+        V("ts", "ei ek", "kw", T.ei[:, 0:24], T.kw[:, 0:24], 3, 15, A.arith_shift_right, A.bitwise_and)
+        V("tr", "t2", "g2_0 g2_1", T.t2[:], T.g2[:])
+        V("tt", "ij", "ei ij", T.ij[:, 12:24], T.ei[:, 12:24], T.ij[:, 12:24], A.subtract)
         V("tt", "w2", "t2", T.w2[:, :, 1:17], T.t2[:, 0:8:2, :], T.t2[:, 1:8:2, :], A.add)
-        for b in range(4):
-            V("ts", "ff%d" % b, "rv ijf", T.ff[:, b, :], T.rv[:, 0:6], T.ijf[:, b:b + 1], None, A.is_le)
+        V("tt", "ff", "rv ij", T.ff[:], T.ij[:], T.rv[:], A.is_ge)
         V("tt", "dd", "w2 w2z", T.dd[:], T.w2[:, :, 1:7], T.w2[:, :, 0:6], A.subtract)
-        V("tt", "d2", "dd ff0 ff1 ff2 ff3", T.d2[:], T.dd[:], T.ff[:], A.mult)
+        V("tt", "d2", "dd ff", T.d2[:], T.dd[:], T.ff[:], A.mult)
         V("scan", "ab", "d2 scab", T.ab[:], T.scab[:], T.d2[:], 0.0, A.mult, A.add)
-        for kind in range(2):
-            for b in range(2):
-                o = 12 * kind
-                V("cp", "ab16_%d%d" % (kind, b), "ab", T.ab16[:, o + b:o + 12:2], T.ab[:, o + 6 * b:o + 6 * b + 6])
+        V("cp", "ab16", "ab cl16", T.ab16[:], T.ab[:, 0:24].indirect(T.cl16[:, 4:6]))
         V("tt", "br", "w2", T.br[:], T.w2[:, 2:4, 16], T.w2[:, 0:2, 16], A.is_gt)
-        V("tt", "dba", "ab", T.dba[:], T.ab[:, 12:24], T.ab[:, 0:12], A.subtract)
-        for b in range(2):
-            V("ts", "bt_%d" % b, "dba br", T.bt[:, 6 * b:6 * b + 6], T.dba[:, 6 * b:6 * b + 6], T.br[:, b:b + 1], None, A.mult)
+        V("tt", "dba", "ab", T.dba[:, 0:12], T.ab[:, 12:24], T.ab[:, 0:12], A.subtract)
+        V("tt", "bt", "dbz dba br cl16", T.bt[:], T.br[:, 0:2].indirect(T.cl16[:, 6:7]), T.dba[:], A.mult)
         for b in range(4):
-            S("at%d" % b, "f2z f2_%d ab16_00 ab16_01" % b, T.at[:, 192 * b:192 * b + 192], T.f2[:, 272 * b:272 * b + 272].indirect(T.ab16[:, 0:12]), ACT.Copy)
-            V("tt", "zt%d" % b, "f2z f2_%d ab16_10 ab16_11 at%d" % (b, b), T.zt[:, b:768:4], T.f2[:, 272 * b:272 * b + 272].indirect(T.ab16[:, 12:24]), T.at[:, 192 * b:192 * b + 192], A.add)
+            S("at%d" % b, "f2z f2_%d ab16" % b, T.at[:, 192 * b:192 * b + 192], T.f2[:, 272 * b:272 * b + 272].indirect(T.ab16[:, 0:12]), ACT.Copy)
+            V("tt", "zt%d" % b, "f2z f2_%d ab16 at%d" % (b, b), T.zt[:, b:768:4], T.f2[:, 272 * b:272 * b + 272].indirect(T.ab16[:, 12:24]), T.at[:, 192 * b:192 * b + 192], A.add)
         V("qz", "zq zp", "zt0 zt1 zt2 zt3", T.zq[:, 0:192], T.zp[:, 0:192], T.zt[:, 0:768])
         send(t)
-        V("tt", "dba", "bt_0 bt_1 ab", T.dba[:], T.bt[:], T.ab[:, 0:12], A.add)
-        for b in range(2):
-            V("cp", "bt16_%d" % b, "dba", T.bt16[:, b:12:2], T.dba[:, 6 * b:6 * b + 6])
-        V("tt", "ke", "bt16_0 bt16_1 w64 kk", T.ke[:], T.w64[:, 0:272].indirect(T.bt16[:, 0:12]), T.kk[:], A.add)
+        V("tt", "d2", "bt ab", T.d2[:, 0:12], T.bt[:, 0:12], T.ab[:, 0:12], A.add)
+        V("cp", "bt16", "d2 cl16", T.bt16[:], T.d2[:, 0:12].indirect(T.cl16[:, 8:9]))
+        V("tt", "ke", "bt16 w512 kk", T.ke[:], T.w512[:, 0:272].indirect(T.bt16[:, 0:12]), T.kk[:], A.add)
         for c in range(16):
-            S("abd%d" % c, "ke n64 abz", T.abd[:, c, 0:192], T.ke[:], ACT.Abs, bias=T.n64[:, c:c + 1], scale=1.0)
-        V("ts", "li0", "kn", T.li[:, 0:2], T.kn[:], 15, None, A.bitwise_and)
-        V("ts", "li1", "kn", T.li[:, 2:4], T.kn[:], 4, None, A.arith_shift_right)
-        V("ts", "li2", "kn", T.li[:, 4:6], T.kn[:], 9, None, A.arith_shift_right)
-        V("ts", "li3", "li0", T.li[:, 6:8], T.li[:, 0:2], 16.0, 256.0, A.mult, A.add)
-        V("ts", "li4", "br", T.li[:, 8:10], T.br[:], -256.0, None, A.mult)
-        V("tt", "li5", "li2 mc", T.li[:, 10:12], T.li[:, 4:6], T.mc[:], A.mult)
-        V("tt", "li6", "li3 li1", T.li[:, 12:14], T.li[:, 6:8], T.li[:, 2:4], A.add)
-        V("tt", "li7", "li4 li5", T.li[:, 14:16], T.li[:, 8:10], T.li[:, 10:12], A.add)
-        V("tt", "li8", "li6 li7", T.li[:, 16:18], T.li[:, 12:14], T.li[:, 14:16], A.add)
-        V("cp", "mt", "idw ab16_00 ab16_01", T.mt[:], T.idw[:, 0:272].indirect(T.ab16[:, 10:12]))
-        V("cp", "ln16", "li8", T.ln16[:], T.li[:, 16:18])
+            S("abd%d" % c, "ke n512 abz", T.abd[:, c, 0:192], T.ke[:], ACT.Abs, bias=T.n512[:, c:c + 1], scale=1.0)
+        V("ts", "li0", "kn", T.li[:, 0:2], T.kn[:, 0:4:2], 15, None, A.bitwise_and)
+        V("ts", "li1", "kn", T.li[:, 2:4], T.kn[:, 0:4:2], 4, None, A.arith_shift_right)
+        V("ts", "li2", "br", T.li[:, 4:6], T.br[:], -256.0, 256.0, A.mult, A.add)
+        V("ts", "li0", "li0", T.li[:, 0:2], T.li[:, 0:2], 16.0, None, A.mult)
+        V("tt", "li1", "li1 li2", T.li[:, 6:8], T.li[:, 2:4], T.li[:, 4:6], A.add)
+        V("cp", "mt", "idw ab16", T.mt[:], T.idw[:, 0:272].indirect(T.ab16[:, 10:12]))
+        V("tt", "li3", "li0 li1", T.li[:, 8:10], T.li[:, 0:2], T.li[:, 6:8], A.add)
+        V("cp", "ln16", "li3", T.ln16[:], T.li[:, 8:10])
         V("cp", "lt0 lt1", "mt ln16", T.lt[:, 0:560].indirect(T.ln16[:, 0:2]), T.mt[:])
         dma("y", "dl0", ["lt0"], ["lw"], T.lw[:, 0:16], T.lt[0:128:16, 0:256])
         dma("y", "dl1", ["lt1"], ["lwb"], T.lw[:, 16:32], T.lt[0:128:16, 256:512])
@@ -351,7 +351,7 @@ def rank_program(g, core, T, topo):
             V("qz", "vq vp", "vt", T.vq[:, 0:128], T.vp[:, 0:128], T.vt[:, 0:512])
         for c in range(16):
             V("red", "ev%d" % c, "abz abd%d" % c, T.ev[:, c:c + 1], T.abd[:, c, 0:193], XAX, A.min)
-        V("ts", "ei", " ".join("ev%d" % c for c in range(16)), T.ei[:, 0:16], T.ev[:], 256.0, None, A.mult)
+        V("ts", "ei", " ".join("ev%d" % c for c in range(16)), T.ei[:, 0:16], T.ev[:], 32.0, None, A.mult)
         V("ts", "ek", "ei", T.ei[:, 16:32], T.ei[:, 0:16], 255, None, A.bitwise_and)
         V("ts", "em", "ei", T.ei[:, 32:48], T.ei[:, 0:16], 8, None, A.arith_shift_right)
         V("tt", "ex2", "ek em", T.ei[:, 48:64], T.ei[:, 16:32], T.ei[:, 32:48], A.add)

import numpy as np
from concourse.mybir import dt, AluOpType, ActivationFunctionType, AxisListType

N = 8
R = 3
C = 256
NS = 11
BIG = 131072.0
F32, BF, I32, U16, U8, X4 = "float32", "bfloat16", "int32", "uint16", "uint8", "float8_e4m3fn_x4"


def _sb(n, d):
    return ("sbuf", [128, n], d)


SCRATCH = {
    "xt": _sb(1024, BF), "xs": _sb(1024, BF), "ut": _sb(512, BF), "vt": _sb(512, BF), "et": _sb(2048, BF),
    "eye": _sb(128, BF), "one": _sb(128, BF),
    "xq": _sb(256, X4), "xp": _sb(256, U8), "uq": _sb(128, X4), "up": _sb(128, U8), "uq2": _sb(128, X4),
    "up2": _sb(128, U8), "vq": _sb(128, X4), "vp": _sb(128, U8), "eq": _sb(512, X4), "ep": _sb(512, U8),
    "wq": _sb(512, X4), "wp": _sb(512, U8),
    "zt": _sb(768, BF), "zq": _sb(192, X4), "zp": _sb(192, U8),
    "pi": _sb(4, I32), "pf": _sb(4, F32), "sm": _sb(64, F32), "idw": _sb(512, F32), "rp": _sb(256, F32), "nmask": _sb(256, F32),
    "sc0": _sb(256, F32), "nw": _sb(16, F32), "nT": _sb(256, F32), "nTi": _sb(256, F32), "kk": _sb(192, F32), "rv": _sb(24, F32),
    "scab": _sb(24, F32), "exl": _sb(16, U16), "upl": _sb(8, U16), "w256": _sb(512, F32), "w2048": _sb(272, F32),
    "w512": _sb(272, F32), "n512": _sb(16, F32), "nm": _sb(2, F32), "md": _sb(576, F32), "gm": _sb(64, F32),
    "cl": _sb(160, F32), "cl2": _sb(160, F32), "cl16": _sb(10, U16),
    "v0": _sb(256, F32), "a1": _sb(256, F32), "a2": _sb(256, F32), "a3": _sb(256, F32), "a4": _sb(256, F32),
    "asc": _sb(256, F32),
    "ms": _sb(256, F32), "sc": _sb(256, F32), "ssb": _sb(256, F32), "cf": _sb(48, F32),
    "wc16": _sb(16, U16), "va": _sb(256, F32), "vb": _sb(256, F32), "pq": _sb(1280, F32),
    "t3": ("sbuf", [128, 32, 16], F32), "e3": ("sbuf", [128, 16, 36], BF), "e2": _sb(576, BF), "so": _sb(576, F32),
    "ne": _sb(32, F32), "yv": _sb(16, F32), "ex": _sb(256, F32),
    "ur": _sb(256, F32), "jk": _sb(4096, BF), "acc": _sb(16, F32), "acc2": _sb(16, F32),
    "a16": _sb(16, U16), "nB": _sb(32, F32), "kap": _sb(256, F32), "r16": _sb(16, U16),
    "qq": _sb(256, F32), "xk0": _sb(264, F32), "xk1": _sb(264, F32), "kv": _sb(2, F32), "kw": _sb(32, I32),
    "kn": _sb(16, I32), "off": _sb(4, U16), "g2": _sb(128, F32), "t2": ("sbuf", [128, 8, 16], F32),
    "w2": ("sbuf", [128, 4, 20], F32), "ij": _sb(24, I32),
    "ff": _sb(24, F32), "dd": _sb(24, F32), "d2": _sb(24, F32), "ab": _sb(24, F32),
    "ab16": _sb(32, U16), "br": _sb(2, F32), "dba": _sb(16, F32), "bt": _sb(16, F32), "bt16": _sb(16, U16),
    "ke": _sb(192, F32), "abd": ("sbuf", [128, 16, 200], F32), "ev": _sb(16, F32), "ei": _sb(64, I32), "e16": _sb(16, U16),
    "li": _sb(12, I32), "ln16": _sb(2, U16), "mt": _sb(32, I32), "lt": _sb(560, I32), "lw": _sb(32, I32),
    "lw16": _sb(32, U16), "dl": _sb(16, F32), "olr": _sb(512, F32), "ysb": _sb(256, F32),
    "at": _sb(768, BF), "f2": _sb(1088, BF), "fw": _sb(1024, BF), "hb": _sb(896, F32),
}
PS = ["ps1", "ps2", "pd0", "pd1", "pd2", "pd3", "ph0", "ph1"]
for _t in range(R):
    SCRATCH["yq%d" % _t] = _sb(192, X4)
    SCRATCH["yp%d" % _t] = _sb(192, U8)
for _n in PS:
    SCRATCH[_n] = ("psum", [128, 512], F32)

DMAS = ["dx", "du", "dv", "dwc", "dws", "dn0", "dn1", "dlt", "das", "dl0", "dl1", "oy", "ool", "ooc", "os0", "os1", "os2", "os3"]
SEMAPHORES = ["sv", "ss", "sp", "sg", "lc"] + ["ar%d" % t for t in range(R)] + DMAS


def rank_program(g, core, T, topo):
    rank = T.rank_of(core)
    if rank is None:
        return
    A = AluOpType
    ACT = ActivationFunctionType
    XAX = AxisListType.X
    queues = {"v": g.vector, "s": g.scalar, "p": g.tensor, "g": g, "y": g.sync}
    total, waited, wr, rd = {}, {q: {} for q in queues}, {}, {}

    def need(q, deps):
        best = {}
        for s, n in deps:
            best[s] = max(best.get(s, 0), n)
        for s in sorted(best):
            if waited[q].get(s, 0) < best[s]:
                queues[q].wait_ge(T.sem[s], best[s])
                waited[q][s] = best[s]

    def before(q, reads, writes):
        deps = []
        for k in reads:
            if k in wr:
                deps.append(wr[k][1:])
            if k in PS:
                deps += [r[1:] for r in rd.get(k, []) if r[0] != q]
        for k in writes:
            if k in wr:
                deps.append(wr[k][1:])
            deps += [r[1:] for r in rd.get(k, [])]
        need(q, deps)

    def after(q, sem, inc, reads, writes):
        total[sem] = total.get(sem, 0) + inc
        tok = (q, sem, total[sem])
        for k in writes:
            wr[k] = tok
            rd[k] = []
        for k in reads:
            if k not in writes:
                rd[k] = [r for r in rd.get(k, []) if r[1] != sem] + [tok]

    def op(q, reads, writes, name, *args, **kw):
        before(q, reads, writes)
        fns = {"memset": g.vector.memset, "tt": g.vector.tensor_tensor, "ts": g.vector.tensor_scalar,
               "cp": g.vector.tensor_copy, "red": g.vector.tensor_reduce, "scan": g.vector.tensor_tensor_scan,
               "tr": g.vector.transpose, "qz": g.vector.quantize_mx, "act": g.scalar.activation,
               "mm": g.tensor.matmul_mx, "iota": g.iota, "asel": g.affine_select}
        fns[name](*args, **kw).then_inc(T.sem["s" + q], 1)
        after(q, "s" + q, 1, reads, writes)

    def dma(q, sem, reads, writes, out, in_):
        before(q, reads, writes)
        queues[q].dma_start(out, in_).then_inc(T.sem[sem], 16)
        after(q, sem, 16, reads, writes)

    def V(name, writes, reads, *args, **kw):
        op("v", reads.split(), writes.split(), name, *args, **kw)

    def S(writes, reads, out, in_, func, **kw):
        op("s", reads.split(), writes.split(), "act", out, in_, func, **kw)

    dma("y", "dx", [], ["xt"], T.xt[:], T.x[:])
    dma("s", "du", [], ["ut"], T.ut[:], T.u[:])
    dma("y", "dn0", [], ["lw", "lwb"], T.lw[:], T.nb[:])
    dma("y", "dn1", [], ["lt0"], T.lt[0:128:16, 0:256], T.nb[:, 0:16])
    dma("y", "dlt", [], ["lt1"], T.lt[0:128:16, 256:512], T.nb[:, 16:32])
    dma("y", "dwc", [], ["wq"], T.wq[:, 0:512].bitcast(dt.uint8), T.wc[:])
    dma("y", "dws", [], ["wp"], T.wp[:, 0:512], T.ws[:])
    dma("y", "dv", [], ["vt"], T.vt[:], T.v[:])

    def iota(key, out, pattern, base, cm=0):
        kw = {} if key == "pi" else {"allow_small_or_imprecise_dtypes": True}
        op("g", [], [key], "iota", out, pattern, base, cm, **kw)
    V("memset", "one", "", T.one[:], 1.0)
    V("memset", "et", "", T.et[:], 0.0)
    iota("pi", T.pi[:, 0:1], [[0, 1]], 0, 1)
    iota("sm1", T.sm[:, 8:14], [[-1, 6]], 5)
    iota("sm2", T.sm[:, 16:22], [[1, 6]], 8)
    iota("sm0", T.sm[:, 0:8], [[16, 8]], 0)
    op("g", ["one"], ["eye"], "asel", T.eye[:], T.one[:], [[-1, 128]], A.is_equal, 0.0, 0, 1)
    iota("idw", T.idw[:], [[1, 512]], 0)
    iota("rp", T.rp[:], [[0, 16], [1, 16]], 0)
    iota("nw0", T.sm[:, 32:48], [[16, 16]], 0)
    iota("exl0", T.sm[:, 48:64], [[1, 16]], 0)
    pairs = [(i, s - i) for s in range(10, 0, -1) for i in range(min(5, s), max(0, s - 5) - 1, -1)]
    worth = [8 * (i + j) + i for i, j in pairs] + [0]
    iota("md", T.md[:], [[0, 576]], -1)
    iota("md", T.md[:, 0:576:36], [[0, 16]], -(2 ** 24 - 1))
    for k in range(len(pairs)):
        d = worth[k] - worth[k + 1]
        if d != 1:
            iota("md", T.md[:, k + 1:576:36], [[0, 16]], -d)
    iota("nTi", T.nTi[:], [[32, 8], [0, 32]], 1)
    iota("w256", T.w256[:], [[256, 512]], -65280)
    iota("w2048", T.w2048[:], [[2048, 272]], 0)
    iota("sm3", T.sm[:, 24:26], [[16, 2]], 0)
    iota("xk0", T.xk0[:, 256:264], [[0, 8]], 527)
    iota("xk1", T.xk1[:, 256:264], [[0, 8]], 783)
    iota("rv", T.rv[:], [[0, 4], [1, 6]], 0)
    iota("gm", T.gm[:], [[0, 2], [1, 2], [0, 16]], 0)
    iota("cl", T.cl[:], [[0, 160]], 0)
    iota("cl", T.cl[:, 0:16], [[0, 4], [1, 2], [0, 2]], 0)
    iota("cl", T.cl[:, 32:56], [[0, 2], [1, 2], [0, 6]], 0)
    iota("cl", T.cl[:, 64:88], [[12, 2], [1, 6], [6, 2]], 0)
    iota("cl", T.cl[:, 96:108], [[1, 2], [0, 6]], 0)
    iota("cl", T.cl[:, 128:140], [[1, 6], [6, 2]], 0)
    iota("pqz", T.pq[:, 512:1280], [[0, 768]], 256)
    for b in range(4):
        iota("f2z", T.f2[:, 272 * b + 256:272 * b + 272], [[0, 16]], 0)
    iota("dbz", T.dba[:, 12:16], [[0, 4]], 0)
    iota("kk", T.kk[:], [[1, 6], [8, 32]], 0)
    iota("w512", T.w512[:], [[512, 272]], 0)
    for b in range(4):
        iota("hbz", T.hb[:, 224 * b + 192:224 * b + 224], [[0, 32]], 0)

    V("ts", "pi1", "pi", T.pi[:, 1:2], T.pi[:, 0:1], 15, None, A.bitwise_and)
    V("ts", "pi2", "pi", T.pi[:, 2:3], T.pi[:, 0:1], 31, None, A.bitwise_and)
    V("ts", "pi3", "pi", T.pi[:, 3:4], T.pi[:, 0:1], 4, 1, A.arith_shift_right, A.bitwise_and)
    V("cp", "pf", "pi1 pi2 pi3", T.pf[:, 0:3], T.pi[:, 1:4])
    r16, p32 = T.pf[:, 0:1], T.pf[:, 1:2]
    V("ts", "sm1", "sm1 pf", T.sm[:, 8:14], T.sm[:, 8:14], r16, None, A.is_equal)
    V("ts", "sm2", "sm2 pf", T.sm[:, 16:22], T.sm[:, 16:22], r16, None, A.is_equal)
    V("cp", "upl", "sm0", T.upl[:], T.sm[:, 0:8])
    V("tt", "sm1", "sm1 sm2", T.sm[:, 8:14], T.sm[:, 8:14], T.sm[:, 16:22], A.add)
    for b in range(4):
        S("et", "eye", T.et[:, 512 * b + b:512 * b + 512:4], T.eye[:], ACT.Copy)
    V("qz", "uq up", "ut", T.uq[:, 0:128], T.up[:, 0:128], T.ut[:, 0:512])
    V("cp", "uq2", "uq upl", T.uq2[:, 0:128].bitcast(dt.uint32), T.uq[:, 0:128].bitcast(dt.uint32).indirect(T.upl[:, 0:8]))
    V("cp", "up2", "up upl", T.up2[:, 0:128], T.up[:, 0:128].indirect(T.upl[:, 0:8]))
    V("qz", "xq xp", "xt", T.xq[:, 0:256], T.xp[:, 0:256], T.xt[:, 0:1024])
    V("ts", "nmask", "rp pf", T.nmask[:], T.rp[:], r16, -1.0, A.is_equal, A.mult)
    V("ts", "sc0", "rp", T.sc0[:], T.rp[:], 0.0, None, A.not_equal)
    for t, k in enumerate(["v0", "a1", "a2", "a3", "a4", "asc"]):
        S(k, "idw sm1", T[k][:], T.idw[:, 0:256], ACT.Copy, scale=T.sm[:, 8 + t:9 + t])

    def lists():
        V("cp", "lw16", "lw lwb", T.lw16[:], T.lw[:])
        V("tt", "dl", "lw lwb", T.dl[:], T.lw[:, 16:32], T.lw[:, 0:16], A.subtract)
    lists()

    def mm(out, st, stk, sc, mv, mvk, mp, n):
        op("p", stk.split() + mvk.split(), [out], "mm", T[out][:, 0:n], st, sc, mv, mp, True, True)

    dst = T.cores[(rank + 1) % N]
    prv = T.cores[(rank - 1) % N]

    def engs(a, b):
        e = topo.engines(a, b)
        return e[::len(e) // 8]
    emask = sum(1 << k for k in engs(core, dst))
    rid, pid = topo.addr(dst)[:2]

    def send(t):
        before("g", ["zq", "zp"], [])
        n = len(engs(core, dst))
        g.remote_dma(T["yq%d" % t][:, 0:192].bitcast(dt.uint8), T.zq[:, 0:192].bitcast(dt.uint8), T.sem["ar%d" % t], T.sem.lc, pid, rid, emask)
        g.remote_dma(T["yp%d" % t][:, 0:192], T.zp[:, 0:192], T.sem["ar%d" % t], T.sem.lc, pid, rid, emask)
        after("g", "lc", 2 * n, ["zq", "zp"], [])
        m = 2 * len(engs(prv, core))
        total["ar%d" % t] = m
        wr["y%d" % t] = ("r", "ar%d" % t, m)

    def late_constants():
        S("md", "md", T.md[:], T.md[:], ACT.Copy, scale=1.0 / 128)
        S("nT", "nTi pf", T.nT[:], T.nTi[:], ACT.Identity, bias=p32, scale=1.0)
        S("nw", "nw0 pf", T.nw[:], T.sm[:, 32:48], ACT.Identity, bias=r16, scale=1.0)
        S("n512", "nw", T.n512[:], T.nw[:], ACT.Copy, scale=-512.0)
        S("sm3", "sm3 pf", T.sm[:, 24:26], T.sm[:, 24:26], ACT.Identity, bias=r16, scale=1.0)
        S("nm", "sm3", T.nm[:], T.sm[:, 24:26], ACT.Copy, scale=-2048.0)
        S("sm4", "pf", T.sm[:, 28:29], r16, ACT.Copy, scale=16.0)
        for k in ("xk0", "xk1"):
            S(k, k + " sm4", T[k][:, 256:264], T[k][:, 256:264], ACT.Identity, bias=T.sm[:, 28:29], scale=1.0)
        V("cp", "exl", "exl0", T.exl[:], T.sm[:, 48:64])

    def later_constants():
        V("ts", "scab", "rv", T.scab[:], T.rv[:], 0.0, None, A.not_equal)
        V("ts", "gm", "gm pf", T.gm[:], T.gm[:], T.pf[:, 2:3], None, A.is_equal)
        V("tt", "cl2", "cl nmask", T.cl2[:], T.cl[:], T.nmask[:, 0:160], A.mult)
        V("scan", "cl", "cl2 sc0", T.cl[:], T.sc0[:, 0:160], T.cl2[:], 0.0, A.mult, A.add)
        V("ts", "cl16", "cl", T.cl16[:], T.cl[:, 15:160:16], -1.0, None, A.mult)
        V("memset", "w2z", "", T.w2[:, :, 0], 0.0)
        V("memset", "abz", "", T.abd[:, :, 192:200], 254.0)
    V("memset", "e3", "", T.e3[:, :, 0], 0.0)

    for t in range(R):
        xq, xp = T.xq[:, 0:256], T.xp[:, 0:256]
        for k in ("ps1", "ps2"):
            mm(k, T.uq2[:, 0:128], "uq2 up2", T.up2[:, 0:128], xq, "xq xp", xp, 256)
        if t == 0:
            V("qz", "eq ep", "et", T.eq[:, 0:512], T.ep[:, 0:512], T.et[:, 0:2048])
        for b in range(4):
            mm("pd%d" % b, T.eq[:, 128 * b:128 * b + 128], "eq ep", T.ep[:, 128 * b:128 * b + 128], xq, "xq xp", xp, 256)
        V("tt", "ms", "ps1 nmask", T.ms[:], T.ps1[:, 0:256], T.nmask[:], A.mult)
        S("ssb", "ps2", T.ssb[:], T.ps2[:, 0:256], ACT.Copy)
        dma("y", "das", ["ssb"], ["asc"], T.asc[15:128:16, :], T.ssb[15:128:16, :])
        V("scan", "sc", "ms sc0", T.sc[:], T.sc0[:], T.ms[:], 0.0, A.mult, A.add)
        V("ts", "cf", "sc", T.cf[:, 0:16], T.sc[:, 15:256:16], 0.0, None, A.is_lt)
        V("tt", "c1", "cf dl", T.cf[:, 16:32], T.cf[:, 0:16], T.dl[:], A.mult)
        V("tt", "c2", "c1 lw lwb", T.cf[:, 32:48], T.cf[:, 16:32], T.lw[:, 0:16], A.add)
        V("cp", "wc16", "c2", T.wc16[:], T.cf[:, 32:48])

        def order(lo, hi):
            for c in range(lo, hi):
                S("jk%d acc%d" % (c, c), "ssb sc", T.jk[:, 256 * c:256 * c + 256], T.ssb[:], ACT.Sign, bias=T.sc[:, 16 * c + 15:16 * c + 16], scale=1.0, accum_out=T.acc[:, c:c + 1])
        order(0, 11)
        cur = "v0"
        for k, add in enumerate(["a1", "a2", "a3", "a4", "asc"]):
            nxt = "va" if k % 2 == 0 else "vb"
            V("tt", nxt, cur + " wc16 " + add, T[nxt][:], T[cur][:, 0:256].indirect(T.wc16[:, 0:16]), T[add][:], A.add)
            cur = nxt
        V("cp", "pq0", cur + " lw16", T.pq[:, 0:256], T[cur][:, 0:256].indirect(T.lw16[:, 0:16]))
        S("pq1", cur + " lw16", T.pq[:, 256:512], T[cur][:, 0:256].indirect(T.lw16[:, 16:32]), ACT.Copy)
        order(11, 16)
        V("tr", "t3", "pq0 pq1", T.t3[:], T.pq[:, 0:512])
        if t == 0:
            late_constants()
        k = 1
        for s in range(10, 0, -1):
            hi, lo = min(5, s), max(0, s - 5)
            n = hi - lo + 1
            V("tt", "e3_%d" % s, "t3 e3", T.e3[:, :, k:k + n], T.t3[:, 0:16, 13 - hi:14 - lo], T.t3[:, 16:32, s - hi:s - lo + 1], A.is_equal)
            k += n
        V("tt", "ne", "t3", T.ne[:, 0:16], T.t3[:, 0:16, 0], T.t3[:, 16:32, 0], A.is_equal)
        V("ts", "e2", "e3 " + " ".join("e3_%d" % s for s in range(1, 11)), T.e2[:], T.e3[:], BIG, 1.0 - BIG, A.mult, A.add)
        V("ts", "neb", "ne", T.ne[:, 16:32], T.ne[:, 0:16], BIG, None, A.mult)
        V("scan", "so", "e2 md", T.so[:], T.e2[:], T.md[:], -BIG, A.max, A.add)
        accs = " ".join("acc%d" % c for c in range(16))
        V("tt", "yv", "neb so", T.yv[:], T.ne[:, 16:32], T.so[:, 35:576:36], A.subtract)
        V("tt", "ex", "yv exl nT", T.ex[:], T.yv[:, 0:16].indirect(T.exl[:, 0:16]), T.nT[:], A.add)
        V("tr", "ur", "ex", T.ur[:], T.ex[:])
        V("ts", "a16", accs, T.a16[:], T.acc[:], 255.0, None, A.add)
        V("ts", "nb0", accs, T.nB[:, 16:32], T.acc[:], -256.0, None, A.mult)
        V("tt", "kap", "a16 w256 ur", T.kap[:], T.w256[:, 0:512].indirect(T.a16[:, 0:16]), T.ur[:], A.add)
        V("tt", "nB", "nb0 nw", T.nB[:, 0:16], T.nB[:, 16:32], T.nw[:], A.subtract)
        for c in range(NS):
            S("jk%d rk%d" % (c, c), "kap nB", T.jk[:, 256 * c:256 * c + 256], T.kap[:], ACT.Sign, bias=T.nB[:, c:c + 1], scale=1.0, accum_out=T.acc2[:, c:c + 1])
        for c in range(NS, 16):
            V("ts", "jk%d" % c, "kap nB", T.jk[:, 256 * c:256 * c + 256], T.kap[:], T.nB[:, c:c + 1], 0.0, A.add, A.is_lt)
        for c in range(NS, 16):
            V("red", "rk%d" % c, "jk%d" % c, T.acc2[:, c:c + 1], T.jk[:, 256 * c:256 * c + 256], XAX, A.add)
        V("cp", "r16b", " ".join("rk%d" % c for c in range(NS, 16)), T.r16[:, NS:16], T.acc2[:, NS:16])
        if t == 0:
            later_constants()
        V("ts", "r16a", " ".join("rk%d" % c for c in range(NS)), T.r16[:, 0:NS], T.acc2[:, 0:NS], -0.5, 128.0, A.mult, A.add)
        V("tt", "qq", "r16a r16b w2048 ur", T.qq[:], T.w2048[:, 0:272].indirect(T.r16[:, 0:16]), T.ur[:], A.add)
        S("xk1a", "qq nm", T.xk1[:, 0:256], T.qq[:], ACT.Identity, bias=T.nm[:, 1:2], scale=1.0)
        V("ts", "xk0a", "qq nm", T.xk0[:, 0:256], T.qq[:], T.nm[:, 0:1], None, A.add)
        V("red", "kv0", "xk0 xk0a", T.kv[:, 0:1], T.xk0[:, 0:264], XAX, A.min, apply_absolute_value=True)
        V("red", "kv1", "xk1 xk1a", T.kv[:, 1:2], T.xk1[:, 0:264], XAX, A.min, apply_absolute_value=True)
        for b in range(4):
            S("f2_%d" % b, "pd%d f2z" % b, T.f2[:, 272 * b:272 * b + 256], T["pd%d" % b][:, 0:256], ACT.Copy, scale=0.5)
        for b in range(4):
            S("fw%d" % b, "pd%d" % b, T.fw[:, 256 * b:256 * b + 256], T["pd%d" % b][:, 0:256], ACT.Copy)
        V("ts", "kn", "kv0 kv1 cl16", T.kn[:], T.kv[:, 0:2].indirect(T.cl16[:, 0:1]), -0.34, None, A.add)
        V("ts", "kw", "kv0 kv1 cl16", T.kw[:], T.kv[:, 0:2].indirect(T.cl16[:, 2:4]), 128.0, None, A.mult)
        V("cp", "off", "kn", T.off[:], T.kn[:, 0:4])
        V("ts", "ij", "kw", T.ij[:], T.kw[:, 0:24], 7, None, A.bitwise_and)
        for kind in range(2):
            V("tt", "g2_%d" % kind, "pqz pq0 pq1 off gm", T.g2[:, 64 * kind:64 * kind + 64], T.pq[:, 256 * kind:256 * kind + 1024].indirect(T.off[:, 0:4]), T.gm[:], A.mult)
        V("ts", "ei ek", "kw", T.ei[:, 0:24], T.kw[:, 0:24], 3, 15, A.arith_shift_right, A.bitwise_and)
        V("tr", "t2", "g2_0 g2_1", T.t2[:], T.g2[:])
        V("tt", "ij", "ei ij", T.ij[:, 12:24], T.ei[:, 12:24], T.ij[:, 12:24], A.subtract)
        V("tt", "w2", "t2", T.w2[:, :, 1:17], T.t2[:, 0:8:2, :], T.t2[:, 1:8:2, :], A.add)
        V("tt", "ff", "rv ij", T.ff[:], T.ij[:], T.rv[:], A.is_ge)
        V("tt", "dd", "w2 w2z", T.dd[:], T.w2[:, :, 1:7], T.w2[:, :, 0:6], A.subtract)
        V("tt", "d2", "dd ff", T.d2[:], T.dd[:], T.ff[:], A.mult)
        V("scan", "ab", "d2 scab", T.ab[:], T.scab[:], T.d2[:], 0.0, A.mult, A.add)
        V("cp", "ab16", "ab cl16", T.ab16[:], T.ab[:, 0:24].indirect(T.cl16[:, 4:6]))
        V("tt", "br", "w2", T.br[:], T.w2[:, 2:4, 16], T.w2[:, 0:2, 16], A.is_gt)
        V("tt", "dba", "ab", T.dba[:, 0:12], T.ab[:, 12:24], T.ab[:, 0:12], A.subtract)
        V("tt", "bt", "dbz dba br cl16", T.bt[:], T.br[:, 0:2].indirect(T.cl16[:, 6:7]), T.dba[:], A.mult)
        for b in range(4):
            S("at%d" % b, "f2z f2_%d ab16" % b, T.at[:, 192 * b:192 * b + 192], T.f2[:, 272 * b:272 * b + 272].indirect(T.ab16[:, 0:12]), ACT.Copy)
            V("tt", "zt%d" % b, "f2z f2_%d ab16 at%d" % (b, b), T.zt[:, b:768:4], T.f2[:, 272 * b:272 * b + 272].indirect(T.ab16[:, 12:24]), T.at[:, 192 * b:192 * b + 192], A.add)
        V("qz", "zq zp", "zt0 zt1 zt2 zt3", T.zq[:, 0:192], T.zp[:, 0:192], T.zt[:, 0:768])
        send(t)
        V("tt", "d2", "bt ab", T.d2[:, 0:12], T.bt[:, 0:12], T.ab[:, 0:12], A.add)
        V("cp", "bt16", "d2 cl16", T.bt16[:], T.d2[:, 0:12].indirect(T.cl16[:, 8:9]))
        V("tt", "ke", "bt16 w512 kk", T.ke[:], T.w512[:, 0:272].indirect(T.bt16[:, 0:12]), T.kk[:], A.add)
        for c in range(16):
            S("abd%d" % c, "ke n512 abz", T.abd[:, c, 0:192], T.ke[:], ACT.Abs, bias=T.n512[:, c:c + 1], scale=1.0)
        V("ts", "li0", "kn", T.li[:, 0:2], T.kn[:, 0:4:2], 15, None, A.bitwise_and)
        V("ts", "li1", "kn", T.li[:, 2:4], T.kn[:, 0:4:2], 4, None, A.arith_shift_right)
        V("ts", "li2", "br", T.li[:, 4:6], T.br[:], -256.0, 256.0, A.mult, A.add)
        V("ts", "li0", "li0", T.li[:, 0:2], T.li[:, 0:2], 16.0, None, A.mult)
        V("tt", "li1", "li1 li2", T.li[:, 6:8], T.li[:, 2:4], T.li[:, 4:6], A.add)
        V("cp", "mt", "idw ab16", T.mt[:], T.idw[:, 0:272].indirect(T.ab16[:, 10:12]))
        V("tt", "li3", "li0 li1", T.li[:, 8:10], T.li[:, 0:2], T.li[:, 6:8], A.add)
        V("cp", "ln16", "li3", T.ln16[:], T.li[:, 8:10])
        V("cp", "lt0 lt1", "mt ln16", T.lt[:, 0:560].indirect(T.ln16[:, 0:2]), T.mt[:])
        dma("y", "dl0", ["lt0"], ["lw"], T.lw[:, 0:16], T.lt[0:128:16, 0:256])
        dma("y", "dl1", ["lt1"], ["lwb"], T.lw[:, 16:32], T.lt[0:128:16, 256:512])
        if t == 0:
            V("qz", "vq vp", "vt", T.vq[:, 0:128], T.vp[:, 0:128], T.vt[:, 0:512])
        for c in range(16):
            V("red", "ev%d" % c, "abz abd%d" % c, T.ev[:, c:c + 1], T.abd[:, c, 0:193], XAX, A.min)
        V("ts", "ei", " ".join("ev%d" % c for c in range(16)), T.ei[:, 0:16], T.ev[:], 32.0, None, A.mult)
        V("ts", "ek", "ei", T.ei[:, 16:32], T.ei[:, 0:16], 255, None, A.bitwise_and)
        V("ts", "em", "ei", T.ei[:, 32:48], T.ei[:, 0:16], 8, None, A.arith_shift_right)
        V("tt", "ex2", "ek em", T.ei[:, 48:64], T.ei[:, 16:32], T.ei[:, 32:48], A.add)
        V("cp", "e16", "ex2", T.e16[:], T.ei[:, 48:64])
        if t == R - 1:
            V("cp", "lw16", "lw lwb", T.lw16[:], T.lw[:])
        ph = ["ph0", "ph1", "ps1", "ps2"]
        for b in range(4):
            mm(ph[b], T.wq[:, 128 * b:128 * b + 128], "wq wp", T.wp[:, 128 * b:128 * b + 128], T["yq%d" % t][:, 0:192], "y%d" % t, T["yp%d" % t][:, 0:192], 192)
            S("hb%d" % b, ph[b] + " hbz", T.hb[:, 224 * b:224 * b + 192], T[ph[b]][:, 0:192], ACT.Copy, scale=0.03125)
            V("tt", "xs%d" % b, "hbz hb%d e16 fw%d" % (b, b), T.xs[:, b:1024:4], T.hb[:, 224 * b:224 * b + 224].indirect(T.e16[:, 0:16]), T.fw[:, 256 * b:256 * b + 256], A.add)
        V("qz", "xq xp", "xs0 xs1 xs2 xs3", T.xq[:, 0:256], T.xp[:, 0:256], T.xs[:, 0:1024])
        if t < R - 1:
            lists()
    S("olr", "idw lw16", T.olr[:], T.idw[:, 0:256].indirect(T.lw16[:, 0:32]), ACT.Copy)
    dma("y", "ool", ["olr"], [], T.ol[:], T.olr[0:128:16, :])
    mm("ps1", T.vq[:, 0:128], "vq vp", T.vp[:, 0:128], T.xq[:, 0:256], "xq xp", T.xp[:, 0:256], 256)
    dma("y", "ooc", ["xq"], [], T.oc[:, 0:1024], T.xq[:, 0:256].bitcast(dt.uint8))
    for k in range(4):
        dma("y", "os%d" % k, ["xp"], [], T.osc[4 * k:4 * k + 4, 0:256], T.xp[32 * k:32 * k + 4, 0:256])
    S("ysb", "ps1", T.ysb[:], T.ps1[:, 0:256], ACT.Copy)
    dma("s", "oy", ["ysb"], [], T.y[:], T.ysb[:])
    need("g", [(s, n) for s, n in total.items()])
